import numpy as np
import ml_dtypes


def mxq(x, axis, fmt="e4m3"):
    dtype, down = {"e4m3": (ml_dtypes.float8_e4m3fn, 7), "e5m2": (ml_dtypes.float8_e5m2, 14)}[fmt]
    v = np.moveaxis(np.asarray(x, np.float32).astype(ml_dtypes.bfloat16).astype(np.float64), axis, -1)
    blocks = v.reshape(v.shape[:-1] + (-1, 32))
    amax = np.abs(blocks).max(-1, keepdims=True)
    byte = np.maximum(np.where(amax > 0, np.frexp(amax)[1] - 1 + 127, 0) - down, 1)
    scale = np.exp2(byte - 127.0)
    codes = (blocks / scale).astype(np.float32).astype(dtype).astype(np.float64)
    return np.moveaxis((codes * scale).reshape(v.shape), -1, axis)


WIDE = False


def mx_kscale(k):
    if not WIDE:
        return np.ones(k)
    levels = np.array([10, -10, 5, -5, 0])
    if k % 512:
        return np.exp2(np.random.permutation(np.resize(levels, k // 32))).repeat(32)
    a = np.empty((k // 512, 16))
    for p in range(k // 512):
        a[p, :8] = np.random.permutation(np.resize(levels, 8))
        for g in range(8):
            far = levels[np.abs(levels - a[p, g]) >= 10]
            a[p, g + 8] = far[np.random.randint(len(far))]
    return np.exp2(a.ravel()).repeat(32)


BF16 = ml_dtypes.bfloat16


def bf(x):
    return np.asarray(x, np.float32).astype(BF16)


def f64(x):
    return np.asarray(x).astype(np.float64)


L, B, S, D, G, W, P = 8, 2, 512, 1024, 4, 4, 3
C = D // G
M = W * L * G
EPS = 1e-6


def draw0():
    s0, s1, s2 = mx_kscale(D), mx_kscale(D), mx_kscale(D)
    gain_factor = np.stack([s0, s1, s2], axis=0)
    root_d = np.sqrt(D)
    return {
        "past": bf(np.random.standard_normal((L, B, S, D))),
        "wa": bf(0.5 * np.random.standard_normal((D, M)) / root_d),
        "bb": bf(0.3 * np.random.standard_normal(M)),
        "gz": bf((1.0 + 0.1 * np.random.standard_normal((P, D))) * gain_factor),
        "wq": bf(np.random.standard_normal((D, D)) / root_d / s0[:, None]),
        "wk": bf(np.random.standard_normal((D, D)) / root_d / s1[:, None]),
        "wv": bf(np.random.standard_normal((D, D)) / root_d / s2[:, None]),
    }


def mix_depth(coef, pg):
    acc = coef[:, :, 0, :, None] * pg[0]
    for l in range(1, pg.shape[0]):
        acc = acc + coef[:, :, l, :, None] * pg[l]
    return acc


def rms_gain(x, gain):
    ms = np.mean(x * x, axis=-1, keepdims=True)
    return x / np.sqrt(ms + EPS) * gain


def core(past, wa, bb, gz, wq, wk, wv):
    past = f64(past)
    gz = f64(gz)
    n_l, n_b, n_s, n_d = past.shape

    dw = past[n_l - 1] @ f64(wa) + f64(bb)
    dw = dw.reshape(n_b, n_s, W, n_l, G)

    pg = past.reshape(n_l, n_b, n_s, G, C)
    z = np.stack([mix_depth(dw[:, :, w], pg) for w in range(W)], axis=0)
    z = z.reshape(W, n_b, n_s, n_d)

    n_0 = rms_gain(z[0], gz[0])
    n_1 = rms_gain(z[1], gz[1])
    n_2 = rms_gain(z[2], gz[2])

    q = mxq(n_0, 2, "e4m3") @ mxq(f64(wq), 0, "e4m3")
    k = mxq(n_1, 2, "e4m3") @ mxq(f64(wk), 0, "e4m3")
    v = mxq(n_2, 2, "e4m3") @ mxq(f64(wv), 0, "e4m3")

    t = 1.0 / (1.0 + np.exp(-q))

    return z[3] + t * k + (1.0 - t) * v


def e4m3fn_bytes(y):
    return np.clip(np.asarray(y, np.float64), -448.0, 448.0).astype(np.float32).astype(ml_dtypes.float8_e4m3fn).view(np.uint8)


def e4m3fn_values(b):
    return np.asarray(b, np.uint8).view(ml_dtypes.float8_e4m3fn).astype(np.float64)


def setup_inputs():
    d = draw0()
    x0 = np.asarray(d['wv']).astype(np.float64)
    s = (np.max(np.abs(x0), axis=(1,), keepdims=True) / 448.0).astype(np.float32)
    out = {}
    for k, v in d.items():
        if k == 'wv':
            out['wv_bytes'] = e4m3fn_bytes(x0 / s.astype(np.float64))
            out['wv_scale'] = s
        else:
            out[k] = v
    return out


def reference(past, wa, bb, gz, wq, wk, wv_bytes, wv_scale):
    return core(past, wa, bb, gz, wq, wk, e4m3fn_values(wv_bytes) * wv_scale.astype(np.float64))

@@ -1,0 +1,486 @@
+from contextlib import ExitStack
+
+import concourse.mybir as mybir
+from concourse.masks import make_identity
+
+L, T, D = 8, 1024, 1024
+G, W = 4, 4
+C = D // G
+M = W * L * G
+EPS = 1e-6
+FLOPS = 2 * T * D * (3 * D + M) + 2 * W * L * T * D
+
+F32 = mybir.dt.float32
+BF16 = mybir.dt.bfloat16
+U32 = mybir.dt.uint32
+U8 = mybir.dt.uint8
+FP8 = mybir.dt.float8_e4m3fn
+FP8X4 = mybir.dt.float8_e4m3fn_x4
+ALU = mybir.AluOpType
+ACT = mybir.ActivationFunctionType
+AX = mybir.AxisListType
+
+P = 128
+HALF = 512
+N_MM = 3
+N_EL = 5
+TG = 16
+V_LAYERS = 3
+MANUAL = True
+ZT = 2
+ZB = 3
+NPROD = 24
+EB = 5
+MB = 23
+V0 = 3
+V1 = 3
+VH = 5
+MSG = 1
+PLAN = 5
+M0 = 14
+M1 = 24
+VA = 2
+VB = 4
+VC = 3
+VD = 4
+SD = 1
+WD = 2
+LM = 4
+ONE = 1
+
+X = (0, "-")
+PLANS = [
+    dict(back=(0, "C"), sq=(1, "B"), rstd=X, rstd2=(1, "B"), norm=(2, "B"), turn=(3, "C"), group=(4, "B"), quant=(5, "A"),
+         proj=(5, "C"), mix=(6, "B"), rback=(4, "C"), resid=(5, "B")),
+    dict(back=(0, "C"), sq=(1, "B"), rstd=X, rstd2=(1, "B"), norm=(2, "E"), turn=(3, "C"), group=(4, "B"), quant=(5, "A"),
+         proj=(5, "C"), mix=(6, "B"), rback=(4, "C"), resid=(5, "B")),
+    dict(back=(0, "C"), sq=(1, "B"), rstd=X, rstd2=(1, "B"), norm=(2, "B"), turn=(2, "D"), group=(3, "B"), quant=(4, "A"),
+         proj=(4, "C"), mix=(5, "B"), rback=(3, "C"), resid=(4, "B")),
+    dict(back=(0, "C"), sq=(1, "A"), rstd=X, rstd2=(1, "A"), norm=(2, "A"), turn=(2, "D"), group=(3, "B"), quant=(4, "A"),
+         proj=(4, "C"), mix=(5, "B"), rback=(3, "C"), resid=(4, "B")),
+    dict(back=(0, "C"), sq=(1, "A"), rstd=X, rstd2=(1, "A"), norm=(2, "A"), turn=(2, "D"), group=(3, "B"), quant=(3, "E"),
+         proj=(4, "C"), mix=(5, "A"), rback=(3, "C"), resid=(4, "B")),
+    dict(back=(0, "C"), sq=(1, "B"), rstd=X, rstd2=(1, "B"), norm=(2, "E"), turn=(3, "C"), group=(4, "A"), quant=(4, "E"),
+         proj=(5, "C"), mix=(6, "A"), rback=(4, "C"), resid=(5, "B")),
+]
+
+
+def tile_muddmultiwaydensegate_kernel(tc, past, wa, bb, gz, wq, wk, wv_bytes, wv_scale, out):
+    nc = tc.nc
+    xs = past.rearrange("l b s d -> l (b s) d")
+    rows = out.rearrange("b s d -> (b s) d")
+
+    with ExitStack() as ctx:
+        keep = ctx.enter_context(tc.tile_pool(name="keep", bufs=1))
+        work = ctx.enter_context(tc.tile_pool(name="work", bufs=2))
+        psum = ctx.enter_context(tc.psum_pool(name="psum", bufs=1))
+        if MANUAL:
+            ctx.enter_context(tc.manual_schedule())
+
+        def bank(tag, shape, dtype=F32):
+            if ONE:
+                return psum.tile(shape, dtype, name=tag, tag="bank", bufs=8)
+            return psum.tile(shape, dtype, name=tag, tag=tag, bufs={"zt": ZT, "z": ZB, "misc": 8 - ZT - ZB}[tag])
+
+        mm_banks, nt_banks, proj, step1, wv_planes, stores = {}, {}, {}, {}, {}, {}
+        x_tiles, dw, coef, diag, zt_mm, raw_mm = {}, {}, {}, {}, {}, {}
+        prods, zt_banks, zt_sb, z_banks, rstd, n_perm, n_grp, n_mx = {}, {}, {}, {}, {}, {}, {}, {}
+        gate, mixed, acc, w_raw, w_grp, w_mx, wide, ssq = {}, {}, {}, {}, {}, {}, {}, {}
+
+        def load_x(i, l):
+            x = work.tile([P, D], BF16, name="x", bufs=18)
+            nc.sync.dma_start(out=x[:], in_=xs[l, i * P:(i + 1) * P, :])
+            x_tiles[i, l] = x
+
+        first = N_MM
+        load_x(first, L - 1)
+        wa_sb = keep.tile([P, D // P, M], BF16, name="wa_sb")
+        nc.sync.dma_start(out=wa_sb[:], in_=wa.rearrange("(j p) m -> p j m", p=P))
+        bias = keep.tile([P, M], BF16, name="bias")
+        nc.sync.dma_start(out=bias[:], in_=bb.partition_broadcast(P))
+        for l in range(L - 1):
+            load_x(first, l)
+
+        ident = keep.tile([P, P], F32, name="ident")
+        make_identity(nc, ident[:])
+        ident_bf = keep.tile([P, P], BF16, name="ident_bf")
+        nc.vector.tensor_copy(out=ident_bf[:], in_=ident[:])
+        own = keep.tile([P, TG], F32, name="own")
+        nc.vector.tensor_reduce(out=own[:], in_=ident[:].rearrange("p (t l) -> p t l", l=L), axis=AX.X, op=ALU.add)
+        minus_half = keep.tile([P, 1], F32, name="minus_half")
+        nc.gpsimd.memset(minus_half[:], -0.5)
+
+        def load_weight(w, h):
+            k_rows = slice(h * HALF, (h + 1) * HALF)
+            if w < 2:
+                raw = work.tile([P, 4, D], BF16, name="raw")
+                nc.sync.dma_start(out=raw[:], in_=(wq, wk)[w][k_rows, :].rearrange("(p j) n -> p j n", j=4))
+            else:
+                raw = work.tile([P, 4 * D], U8, name="wv_codes", bufs=1)
+                nc.sync.dma_start(out=raw[:], in_=wv_bytes[k_rows, :].rearrange("(p j) n -> p (j n)", j=4))
+            w_raw[w, h] = raw
+
+        def widen_wv(h, c):
+            planes = work.tile([P, 4, HALF], BF16, name="wide", align_bytes=64, bufs=4)
+            for j in range(4):
+                col = j * D + c * HALF
+                nc.scalar.activation(out=planes[:, j, :], in_=w_raw[2, h][:, col:col + HALF].bitcast(FP8),
+                                     func=ACT.Copy, scale=neg_scale[:, 4 * h + j:4 * h + j + 1])
+            wv_planes[h, c] = planes
+
+        def interleave_weight(w, h, c):
+            grp = work.tile([P, HALF, 4], BF16, name="wide", align_bytes=64, bufs=4)
+            src = w_raw[w, h][:, :, c * HALF:(c + 1) * HALF] if w < 2 else wv_planes[h, c][:]
+            nc.vector.tensor_copy(out=grp[:].rearrange("p (c i) j -> p c j i", i=4),
+                                  in_=src.rearrange("p j (c i) -> p c j i", i=4))
+            w_grp[w, h, c] = grp
+
+        def quantize_weight(w, h, c):
+            codes = keep.tile([P, HALF], U32, name="w_codes_%d%d%d" % (w, h, c), align_bytes=64)
+            scales = keep.tile([P, HALF], U8, name="w_scales_%d%d%d" % (w, h, c), align_bytes=64)
+            nc.vector.quantize_mx(out=codes[:].bitcast(FP8X4), scales=scales[:],
+                                  in_=w_grp[w, h, c][:].rearrange("p c j -> p (c j)"))
+            w_mx[w, h, c] = (codes, scales)
+
+        def depth_turn(i):
+            xt_ps = bank("misc", [P, D // P, P], BF16)
+            for j in range(D // P):
+                nc.tensor.transpose(xt_ps[:, j, :], x_tiles[i, L - 1][:, j * P:(j + 1) * P], ident_bf[:])
+            step1[i] = xt_ps
+
+        def depth_copy(i):
+            xt = work.tile([P, D // P, P], BF16, name="xt", bufs=1)
+            nc.scalar.copy(out=xt[:], in_=step1[i][:])
+            step1[i] = xt
+
+        def depth_matmul(i):
+            dw_ps = bank("misc", [P, M])
+            for j in range(D // P):
+                nc.tensor.matmul(dw_ps[:], lhsT=step1[i][:, j, :], rhs=wa_sb[:, j, :], start=(j == 0), stop=(j == D // P - 1))
+            step1[i] = dw_ps
+
+        def depth_bias(i):
+            dw_ps = step1[i]
+            d = work.tile([P, M], F32, name="dw", bufs=3)
+            if i >= N_MM:
+                nc.vector.tensor_tensor(out=d[:], in0=dw_ps[:], in1=bias[:], op=ALU.add)
+            else:
+                nc.vector.tensor_tensor(out=d[:].rearrange("p (s w) -> p s w", w=W),
+                                        in0=dw_ps[:].rearrange("p (w s) -> p s w", w=W),
+                                        in1=bias[:].rearrange("p (w s) -> p s w", w=W), op=ALU.add)
+            dw[i] = d
+
+        def regroup_weights(i):
+            park = rows[i * P:i * P + P * M // D, :].rearrange("a (b m) -> (a b) m", m=M)
+            nc.sync.dma_start(out=park, in_=dw[i][:])
+            cf = work.tile([P, P // TG, G * W], F32, name="coef")
+            nc.sync.dma_start(out=cf[:], in_=park.rearrange("(u t) (l x) -> (t l) u x", t=TG, l=L))
+            coef[i] = cf
+
+        def build_diag(i):
+            dg = work.tile([P, P // TG * G, TG, W], F32, name="diag", bufs=1)
+            for t in range(TG):
+                nc.vector.tensor_scalar(out=dg[:, :, t, :], in0=coef[i][:].rearrange("p u (g w) -> p (u g) w", w=W),
+                                        scalar1=own[:, t:t + 1], scalar2=None, op0=ALU.mult)
+            diag[i] = dg
+            zt_mm[i] = work.tile([P, W, D // P, P], F32, name="zt_mm")
+
+        def load_mm(i, h):
+            raw = work.tile([P, P // TG, HALF], BF16, name="raw")
+            for u in range(P // TG):
+                tok = slice(i * P + u * TG, i * P + (u + 1) * TG)
+                nc.sync.dma_start(out=raw[:, u, :], in_=xs[:, tok, h * HALF:(h + 1) * HALF].rearrange("l t d -> t l d"))
+            raw_mm[i, h] = raw
+
+        def widen_chunk(i, j):
+            wd = work.tile([P, P // TG, P], F32, name="wide", align_bytes=64, bufs=4)
+            col = (j % 4) * P
+            nc.vector.tensor_copy(out=wd[:], in_=raw_mm[i, j // 4][:, :, col:col + P])
+            wide[i, j] = wd
+
+        def mix_chunk(i, j):
+            ps = bank("zt", [P, P // TG, TG * W])
+            for u in range(P // TG):
+                nc.tensor.matmul(ps[:, u, :], lhsT=wide[i, j][:, u, :],
+                                 rhs=diag[i][:, u * G + j // 2, :, :].rearrange("p t w -> p (t w)"), start=True, stop=True)
+            mm_banks[i, j] = ps
+
+        def empty_chunk(i, j):
+            nc.scalar.copy(out=zt_mm[i][:, :, j, :], in_=mm_banks[i, j][:].rearrange("p u (t w) -> p w (u t)", w=W))
+
+        def products(i, w, g, n_vec):
+            for l in range(L):
+                pr = work.tile([P, C], F32, name="prod", bufs=NPROD)
+                col = (w * L + l) * G + g
+                src = x_tiles[i, l][:, g * C:(g + 1) * C]
+                if l < n_vec:
+                    nc.vector.tensor_scalar(out=pr[:], in0=src, scalar1=dw[i][:, col:col + 1], scalar2=None, op0=ALU.mult)
+                else:
+                    nc.scalar.activation(out=pr[:], in_=src, func=ACT.Copy, scale=dw[i][:, col:col + 1])
+                prods[i, w, g, l] = pr
+
+        def add_layers(i, w, g):
+            if g % 2 == 0:
+                zt_banks[i, w, g // 2] = bank("zt", [P, 4, P])
+            ps = zt_banks[i, w, g // 2]
+            for c in range(2):
+                for l in range(L):
+                    nc.tensor.matmul(ps[:, 2 * (g % 2) + c, :], lhsT=prods[i, w, g, l][:, c * P:(c + 1) * P], rhs=ident[:],
+                                     is_transpose=True, start=(l == 0), stop=(l == L - 1))
+
+        def empty_sums(i, w, h):
+            sb = work.tile([P, 4, P], F32, name="zt_el", bufs=3)
+            nc.scalar.copy(out=sb[:], in_=zt_banks[i, w, h][:])
+            zt_sb[i, w, h] = sb
+
+        def chain(i, l, g):
+            if l == 0 and g == 0:
+                acc[i] = work.tile([P, D], F32, name="acc")
+            col = ((W - 1) * L + l) * G + g
+            cols = slice(g * C, (g + 1) * C)
+            if l == 0:
+                nc.vector.tensor_scalar(out=acc[i][:, cols], in0=x_tiles[i, l][:, cols], scalar1=dw[i][:, col:col + 1],
+                                        scalar2=None, op0=ALU.mult)
+            else:
+                nc.vector.scalar_tensor_tensor(out=acc[i][:, cols], in0=x_tiles[i, l][:, cols], scalar=dw[i][:, col:col + 1],
+                                               in1=acc[i][:, cols], op0=ALU.mult, op1=ALU.add)
+
+        def turn_back(i, w, h, tag):
+            ps = bank(tag, [P, 4, P])
+            for c in range(4):
+                src = zt_mm[i][:, w, 4 * h + c, :] if i < N_MM else zt_sb[i, w, h][:, c, :]
+                nc.tensor.transpose(ps[:, c, :], src, ident[:])
+            return ps[:].rearrange("p c k -> p (c k)")
+
+        def stage_back(i, w):
+            for h in range(2):
+                z_banks[i, w, h] = turn_back(i, w, h, "z")
+
+        def stage_squares(i, w):
+            ss = work.tile([P, 2], F32, name="ss", bufs=3)
+            for h in range(2):
+                junk = work.tile([P, HALF], BF16, name="squares")
+                nc.scalar.activation(out=junk[:], in_=z_banks[i, w, h], func=ACT.Square, scale=D ** -0.5,
+                                     accum_out=ss[:, h:h + 1])
+            ssq[i, w] = ss
+
+        def stage_rstd(i, w):
+            ms = work.tile([P, 1], F32, name="ms", bufs=3)
+            (nc.gpsimd if MSG else nc.vector).tensor_scalar(out=ms[:], in0=ssq[i, w][:, 0:1], scalar1=ssq[i, w][:, 1:2], scalar2=EPS,
+                                    op0=ALU.add, op1=ALU.add)
+            r = work.tile([P, 1], F32, name="rstd", bufs=3)
+            nc.gpsimd.tensor_tensor(out=r[:], in0=ms[:], in1=minus_half[:], op=ALU.pow)
+            rstd[i, w] = r
+
+        def stage_norm(i, w):
+            n = work.tile([P, 2, 2, P, 2], BF16, name="n_perm")
+            for h in range(2):
+                for u in range(2):
+                    nc.vector.scalar_tensor_tensor(
+                        out=n[:, h, u, :, :],
+                        in0=z_banks[i, w, h].rearrange("t (p u e) -> t u p e", u=2, e=2)[:, u, :, :],
+                        scalar=rstd[i, w][:],
+                        in1=gain[w][:, h * HALF:(h + 1) * HALF].rearrange("t (p u e) -> t u p e", u=2, e=2)[:, u, :, :],
+                        op0=ALU.mult, op1=ALU.mult)
+            n_perm[i, w] = n
+
+        def stage_turn(i, w):
+            words = n_perm[i, w][:].rearrange("t h u p e -> t (h u p e)").bitcast(F32)
+            ps = bank("misc", [P, 2, 2, P])
+            for h in range(2):
+                for u in range(2):
+                    s = 2 * h + u
+                    nc.tensor.transpose(ps[:, h, u, :], words[:, s * P:(s + 1) * P], ident[:])
+            nt_banks[i, w] = ps
+
+        def stage_group(i, w):
+            ps = nt_banks[i, w]
+            grp = work.tile([P, D], BF16, name="n_grp", align_bytes=64)
+            nc.scalar.copy(out=grp[:].bitcast(F32).rearrange("p (h t u) -> p h t u", h=2, u=2),
+                           in_=ps[:].rearrange("p h u t -> p h t u"))
+            n_grp[i, w] = grp
+
+        def stage_quantize(i, w):
+            codes = work.tile([P, 2 * P], U32, name="n_codes", align_bytes=64)
+            scales = work.tile([P, 2 * P], U8, name="n_scales", align_bytes=64)
+            nc.vector.quantize_mx(out=codes[:].bitcast(FP8X4), scales=scales[:], in_=n_grp[i, w][:])
+            n_mx[i, w] = (codes, scales)
+
+        def stage_project(i, w):
+            codes, scales = n_mx[i, w]
+            for c in range(2):
+                ps = bank("misc", [P, HALF])
+                for h in range(2):
+                    nc.tensor.matmul_mx(out=ps[:], lhsT=codes[:, h * P:(h + 1) * P].bitcast(FP8X4),
+                                        lhsT_scale=scales[:, h * P:(h + 1) * P],
+                                        rhs=w_mx[w, h, c][0][:].bitcast(FP8X4), rhs_scale=w_mx[w, h, c][1][:],
+                                        start=(h == 0), stop=(h == 1))
+                proj[i, w, c] = ps
+
+        def stage_mix(i, w):
+            if w == 0:
+                gate[i] = work.tile([P, D], F32, name="gate", bufs=3)
+            if w == 1:
+                mixed[i] = work.tile([P, D], F32, name="mixed", bufs=3)
+            res = []
+            for c in range(2):
+                ps = proj[i, w, c]
+                cols = slice(c * HALF, (c + 1) * HALF)
+                if w == 0:
+                    nc.scalar.activation(out=gate[i][:, cols], in_=ps[:], func=ACT.Sigmoid)
+                elif w == 1:
+                    nc.vector.tensor_tensor(out=mixed[i][:, cols], in0=ps[:], in1=gate[i][:, cols], op=ALU.mult)
+                else:
+                    b = work.tile([P, HALF], F32, name="rest")
+                    nc.vector.scalar_tensor_tensor(out=b[:], in0=gate[i][:, cols], scalar=1.0, in1=ps[:],
+                                                   op0=ALU.subtract, op1=ALU.mult)
+                    res.append(b)
+            for c in range(len(res)):
+                cols = slice(c * HALF, (c + 1) * HALF)
+                nc.vector.tensor_tensor(out=mixed[i][:, cols], in0=mixed[i][:, cols], in1=res[c][:], op=ALU.add)
+            if w == 2:
+                stores[q] = i
+
+        def store(i):
+            for c in range(2):
+                cols = slice(c * HALF, (c + 1) * HALF)
+                nc.sync.dma_start(out=rows[i * P:(i + 1) * P, cols], in_=mixed[i][:, cols])
+
+        def stage_back_residual(i):
+            for c in range(2):
+                z_banks[i, W - 1, c] = turn_back(i, W - 1, c, "misc")
+
+        def stage_residual(i):
+            for c in range(2):
+                cols = slice(c * HALF, (c + 1) * HALF)
+                z3 = z_banks[i, W - 1, c] if i < N_MM else acc[i][:, cols]
+                nc.vector.tensor_tensor(out=mixed[i][:, cols], in0=z3, in1=mixed[i][:, cols], op=ALU.add)
+
+        depth_turn(first)
+        depth_copy(first)
+        depth_matmul(first)
+        depth_bias(first)
+        load_weight(0, 0)
+        load_weight(0, 1)
+        gain = []
+        for w in range(3):
+            gw = keep.tile([P, D], BF16, name="gain_%d" % w)
+            nc.sync.dma_start(out=gw[:], in_=gz[w, :].partition_broadcast(P))
+            gain.append(gw)
+        scale_sb = keep.tile([P, 2, 4], F32, name="scale_sb")
+        nc.sync.dma_start(out=scale_sb[:], in_=wv_scale.rearrange("(h p j) o -> p h (j o)", h=2, j=4))
+        neg_scale = keep.tile([P, 8], F32, name="neg_scale")
+
+        items = {}
+        for r in range(3 * N_EL):
+            items[4 * r + EB] = (N_MM + r // 3, r % 3)
+        for r in range(3 * N_MM):
+            items[4 * r + MB] = (r // 3, r % 3)
+        n_mix = 4 * 3 * N_EL
+        starts = (M0, M1, MB + 12, MB + 24)
+        chunks = {}
+        for i in range(N_MM):
+            for j in range(8):
+                chunks[starts[i] + j * (starts[i + 1] - starts[i]) // 8] = (i, j)
+        depth = {12 * i + 3: i for i in range(N_MM)}
+        for k in range(1, N_EL):
+            depth[12 * k - 5] = N_MM + k
+        for q in range(n_mix + EB + 6):
+            r, g = divmod(q, 4)
+            k, w = divmod(r, 3)
+            tq = q % 12
+            el = N_MM + k
+            if q < n_mix and tq == 2 and k + 1 < N_EL:
+                load_x(el + 1, L - 1)
+            if q < n_mix and tq == 3 and k + 1 < N_EL:
+                for l in range(L - 1):
+                    load_x(el + 1, l)
+            if q in (3, 5):
+                load_weight(1, (q - 3) // 2)
+            if q in (6, 10):
+                load_weight(2, (q - 6) // 4)
+            if q + 2 in depth and depth[q + 2] < N_MM:
+                load_x(depth[q + 2], L - 1)
+            if q + LM in starts[:N_MM]:
+                load_mm(starts.index(q + LM), 0)
+            if q + LM - 4 in starts[:N_MM]:
+                load_mm(starts.index(q + LM - 4), 1)
+            def at(name, fn):
+                off, ph = PLANS[PLAN][name]
+                if ph == phase and q - off in items:
+                    fn(*items[q - off])
+
+            def resid_back(i, w):
+                if w == 2 and i < N_MM:
+                    stage_back_residual(i)
+
+            def resid(i, w):
+                if w == 2:
+                    stage_residual(i)
+
+            def stages():
+                at("rstd", stage_rstd)
+                at("mix", stage_mix)
+                at("norm", stage_norm)
+                at("group", stage_group)
+                at("quant", stage_quantize)
+                at("turn", stage_turn)
+                at("back", stage_back)
+                at("rback", resid_back)
+                at("resid", resid)
+                at("proj", stage_project)
+                at("sq", stage_squares)
+                at("rstd2", stage_rstd)
+
+            if q - SD in stores:
+                store(stores[q - SD])
+            phase = "A"
+            if 1 <= q <= n_mix:
+                pr, pg = divmod(q - 1, 4)
+                add_layers(N_MM + pr // 3, pr % 3, pg)
+            stages()
+            if q == 6:
+                nc.vector.tensor_scalar(out=neg_scale[:], in0=scale_sb[:].rearrange("p h j -> p (h j)"), scalar1=-1.0,
+                                        scalar2=None, op0=ALU.mult)
+            if q < n_mix:
+                products(el, w, g, VH if q < 1 else VA if q < 13 else VB if q < MB else VC if q < MB + 24 else VD)
+            phase = "B"
+            if q - 1 in chunks:
+                empty_chunk(*chunks[q - 1])
+            stages()
+            if q - 1 in depth:
+                depth_copy(depth[q - 1])
+            if q - 3 in depth:
+                depth_bias(depth[q - 3])
+                if depth[q - 3] < N_MM:
+                    regroup_weights(depth[q - 3])
+            if 2 <= q <= n_mix and q % 2 == 0:
+                pr, pg = divmod(q - 1, 4)
+                empty_sums(N_MM + pr // 3, pr % 3, pg // 2)
+            phase = "C"
+            stages()
+            if q in depth:
+                depth_turn(depth[q])
+            if q - 2 in depth:
+                depth_matmul(depth[q - 2])
+            if q in chunks:
+                mix_chunk(*chunks[q])
+            phase = "D"
+            stages()
+            if q < n_mix:
+                for s in range(32 * tq // 12, 32 * (tq + 1) // 12):
+                    chain(el, s // G, s % G)
+            phase = "E"
+            stages()
+            if 2 <= q <= 13:
+                s = q - 2
+                quantize_weight(s // 4, s % 4 // 2, s % 2)
+            if 1 <= q <= 12:
+                s = q - 1
+                interleave_weight(s // 4, s % 4 // 2, s % 2)
+            if 8 <= q <= 11:
+                widen_wv((q - 8) // 2, q % 2)
+            if q + WD in chunks:
+                widen_chunk(*chunks[q + WD])
+            if q + 1 in starts[:N_MM]:
+                build_diag(starts.index(q + 1))

@@ -29,39 +29,59 @@ V_LAYERS = 3
 MANUAL = True
 ZT = 2
 ZB = 3
-NPROD = 24
+NPROD = 20
 EB = 5
-MB = 23
+MB = 25
 V0 = 3
 V1 = 3
 VH = 5
-MSG = 1
-PLAN = 5
-M0 = 14
+MSG = 0
+PLAN = 4
+M0 = 12
 M1 = 24
 VA = 2
-VB = 4
-VC = 3
-VD = 4
+VB = 3
+VC = 2
+VD = 3
 SD = 1
 WD = 2
 LM = 4
+P0 = 10
+PE = 50
+LX = 4
+TL = 0
+VT = 0
+RL = 4
+CE = 3
+DV = 1
+CH = 0
+CL = 12
+HD = 0
+NW = 5
+BD = 2
+RG = 4
 ONE = 1
 
 X = (0, "-")
 PLANS = [
-    dict(back=(0, "C"), sq=(1, "B"), rstd=X, rstd2=(1, "B"), norm=(2, "B"), turn=(3, "C"), group=(4, "B"), quant=(5, "A"),
-         proj=(5, "C"), mix=(6, "B"), rback=(4, "C"), resid=(5, "B")),
-    dict(back=(0, "C"), sq=(1, "B"), rstd=X, rstd2=(1, "B"), norm=(2, "E"), turn=(3, "C"), group=(4, "B"), quant=(5, "A"),
-         proj=(5, "C"), mix=(6, "B"), rback=(4, "C"), resid=(5, "B")),
-    dict(back=(0, "C"), sq=(1, "B"), rstd=X, rstd2=(1, "B"), norm=(2, "B"), turn=(2, "D"), group=(3, "B"), quant=(4, "A"),
-         proj=(4, "C"), mix=(5, "B"), rback=(3, "C"), resid=(4, "B")),
-    dict(back=(0, "C"), sq=(1, "A"), rstd=X, rstd2=(1, "A"), norm=(2, "A"), turn=(2, "D"), group=(3, "B"), quant=(4, "A"),
-         proj=(4, "C"), mix=(5, "B"), rback=(3, "C"), resid=(4, "B")),
-    dict(back=(0, "C"), sq=(1, "A"), rstd=X, rstd2=(1, "A"), norm=(2, "A"), turn=(2, "D"), group=(3, "B"), quant=(3, "E"),
-         proj=(4, "C"), mix=(5, "A"), rback=(3, "C"), resid=(4, "B")),
     dict(back=(0, "C"), sq=(1, "B"), rstd=X, rstd2=(1, "B"), norm=(2, "E"), turn=(3, "C"), group=(4, "A"), quant=(4, "E"),
-         proj=(5, "C"), mix=(6, "A"), rback=(4, "C"), resid=(5, "B")),
+         proj=(5, "C"), mix=(6, "A"), rback=(4, "C"), resid=(5, "B"), rlast=(RL, "D")),
+    dict(back=(0, "C"), sq=(1, "B"), rstd=(2, "A"), rstd2=X, norm=(2, "E"), turn=(3, "C"), group=(4, "A"), quant=(4, "E"),
+         proj=(5, "C"), mix=(6, "A"), rback=(4, "C"), resid=(5, "B"), rlast=(RL, "D")),
+    dict(back=(0, "C"), sq=(1, "A"), rstd=(1, "E"), rstd2=X, norm=(2, "B"), turn=(3, "C"), group=(4, "A"), quant=(4, "E"),
+         proj=(5, "C"), mix=(6, "A"), rback=(4, "C"), resid=(5, "B"), rlast=(RL, "D")),
+    dict(back=(0, "C"), sq=(1, "A"), rstd=(1, "E"), rstd2=X, norm=(2, "B"), turn=(2, "D"), group=(3, "B"), quant=(4, "A"),
+         proj=(4, "C"), mix=(5, "E"), rback=(3, "C"), resid=(4, "B"), rlast=(RL, "D")),
+    dict(back=(0, "C"), sq=(1, "A"), rstd=(2, "A"), rstd2=X, norm=(2, "E"), turn=(3, "C"), group=(4, "A"), quant=(4, "E"),
+         proj=(5, "C"), mix=(6, "A"), rback=(4, "C"), resid=(5, "B"), rlast=(RL, "D")),
+    dict(back=(0, "C"), sq=(1, "A"), rstd=(2, "A"), rstd2=X, norm=(2, "D"), turn=(3, "C"), group=(4, "A"), quant=(4, "E"),
+         proj=(5, "C"), mix=(6, "A"), rback=(4, "C"), resid=(5, "B"), rlast=(RL, "D")),
+    dict(back=(0, "C"), sq=(1, "A"), rstd=(1, "E"), rstd2=X, norm=(2, "B"), turn=(2, "D"), group=(3, "A"), quant=(3, "E"),
+         proj=(4, "C"), mix=(5, "E"), rback=(4, "C"), resid=(5, "B"), rlast=(RL, "D")),
+    dict(back=(0, "C"), sq=(1, "A"), rstd=(1, "E"), rstd2=X, norm=(2, "E"), turn=(3, "C"), group=(4, "A"), quant=(4, "B"),
+         proj=(4, "D"), mix=(5, "E"), rback=(4, "C"), resid=(5, "B"), rlast=(RL, "D")),
+    dict(back=(0, "C"), sq=(1, "A"), rstd=(2, "B"), rstd2=X, norm=(2, "E"), turn=(3, "C"), group=(4, "A"), quant=(4, "E"),
+         proj=(5, "C"), mix=(6, "B"), rback=(4, "C"), resid=(5, "B"), rlast=(RL, "D")),
 ]
 
 
@@ -98,9 +118,6 @@ def tile_muddmultiwaydensegate_kernel(tc, past, wa, bb, gz, wq, wk, wv_bytes, wv
         nc.sync.dma_start(out=wa_sb[:], in_=wa.rearrange("(j p) m -> p j m", p=P))
         bias = keep.tile([P, M], BF16, name="bias")
         nc.sync.dma_start(out=bias[:], in_=bb.partition_broadcast(P))
-        for l in range(L - 1):
-            load_x(first, l)
-
         ident = keep.tile([P, P], F32, name="ident")
         make_identity(nc, ident[:])
         ident_bf = keep.tile([P, P], BF16, name="ident_bf")
@@ -110,18 +127,19 @@ def tile_muddmultiwaydensegate_kernel(tc, past, wa, bb, gz, wq, wk, wv_bytes, wv
         minus_half = keep.tile([P, 1], F32, name="minus_half")
         nc.gpsimd.memset(minus_half[:], -0.5)
 
-        def load_weight(w, h):
-            k_rows = slice(h * HALF, (h + 1) * HALF)
-            if w < 2:
-                raw = work.tile([P, 4, D], BF16, name="raw")
-                nc.sync.dma_start(out=raw[:], in_=(wq, wk)[w][k_rows, :].rearrange("(p j) n -> p j n", j=4))
-            else:
-                raw = work.tile([P, 4 * D], U8, name="wv_codes", bufs=1)
-                nc.sync.dma_start(out=raw[:], in_=wv_bytes[k_rows, :].rearrange("(p j) n -> p (j n)", j=4))
-            w_raw[w, h] = raw
+        def load_weight(w, h, c):
+            raw = work.tile([P, 4, HALF], BF16, name="raw", bufs=4)
+            src = (wq, wk)[w][h * HALF:(h + 1) * HALF, c * HALF:(c + 1) * HALF]
+            nc.sync.dma_start(out=raw[:], in_=src.rearrange("(p j) n -> p j n", j=4))
+            w_raw[w, h, c] = raw
+
+        def load_wv(h):
+            raw = work.tile([P, 4 * D], U8, name="wv_codes", bufs=2)
+            nc.sync.dma_start(out=raw[:], in_=wv_bytes[h * HALF:(h + 1) * HALF, :].rearrange("(p j) n -> p (j n)", j=4))
+            w_raw[2, h] = raw
 
         def widen_wv(h, c):
-            planes = work.tile([P, 4, HALF], BF16, name="wide", align_bytes=64, bufs=4)
+            planes = work.tile([P, 4, HALF], BF16, name="wide", align_bytes=64, bufs=NW)
             for j in range(4):
                 col = j * D + c * HALF
                 nc.scalar.activation(out=planes[:, j, :], in_=w_raw[2, h][:, col:col + HALF].bitcast(FP8),
@@ -129,8 +147,8 @@ def tile_muddmultiwaydensegate_kernel(tc, past, wa, bb, gz, wq, wk, wv_bytes, wv
             wv_planes[h, c] = planes
 
         def interleave_weight(w, h, c):
-            grp = work.tile([P, HALF, 4], BF16, name="wide", align_bytes=64, bufs=4)
-            src = w_raw[w, h][:, :, c * HALF:(c + 1) * HALF] if w < 2 else wv_planes[h, c][:]
+            grp = work.tile([P, HALF, 4], BF16, name="wide", align_bytes=64, bufs=NW)
+            src = w_raw[w, h, c][:] if w < 2 else wv_planes[h, c][:]
             nc.vector.tensor_copy(out=grp[:].rearrange("p (c i) j -> p c j i", i=4),
                                   in_=src.rearrange("p j (c i) -> p c j i", i=4))
             w_grp[w, h, c] = grp
@@ -173,42 +191,48 @@ def tile_muddmultiwaydensegate_kernel(tc, past, wa, bb, gz, wq, wk, wv_bytes, wv
         def regroup_weights(i):
             park = rows[i * P:i * P + P * M // D, :].rearrange("a (b m) -> (a b) m", m=M)
             nc.sync.dma_start(out=park, in_=dw[i][:])
+
+        def fetch_weights(i):
+            park = rows[i * P:i * P + P * M // D, :].rearrange("a (b m) -> (a b) m", m=M)
             cf = work.tile([P, P // TG, G * W], F32, name="coef")
             nc.sync.dma_start(out=cf[:], in_=park.rearrange("(u t) (l x) -> (t l) u x", t=TG, l=L))
             coef[i] = cf
 
-        def build_diag(i):
-            dg = work.tile([P, P // TG * G, TG, W], F32, name="diag", bufs=1)
-            for t in range(TG):
-                nc.vector.tensor_scalar(out=dg[:, :, t, :], in0=coef[i][:].rearrange("p u (g w) -> p (u g) w", w=W),
-                                        scalar1=own[:, t:t + 1], scalar2=None, op0=ALU.mult)
-            diag[i] = dg
-            zt_mm[i] = work.tile([P, W, D // P, P], F32, name="zt_mm")
+        def build_diag(i, g):
+            dg = work.tile([P, P // TG, TG, W], F32, name="diag")
+            shape = [P, P // TG, TG, W]
+            nc.vector.tensor_tensor(out=dg[:], in0=coef[i][:, :, g * W:(g + 1) * W].unsqueeze(2).to_broadcast(shape),
+                                    in1=own[:].unsqueeze(1).unsqueeze(3).to_broadcast(shape), op=ALU.mult)
+            diag[i, g] = dg
 
-        def load_mm(i, h):
-            raw = work.tile([P, P // TG, HALF], BF16, name="raw")
+        def load_mm(i, g):
+            raw = work.tile([P, P // TG, C], BF16, name="raw", bufs=4)
             for u in range(P // TG):
                 tok = slice(i * P + u * TG, i * P + (u + 1) * TG)
-                nc.sync.dma_start(out=raw[:, u, :], in_=xs[:, tok, h * HALF:(h + 1) * HALF].rearrange("l t d -> t l d"))
-            raw_mm[i, h] = raw
+                nc.sync.dma_start(out=raw[:, u, :], in_=xs[:, tok, g * C:(g + 1) * C].rearrange("l t d -> t l d"))
+            raw_mm[i, g] = raw
 
         def widen_chunk(i, j):
-            wd = work.tile([P, P // TG, P], F32, name="wide", align_bytes=64, bufs=4)
-            col = (j % 4) * P
-            nc.vector.tensor_copy(out=wd[:], in_=raw_mm[i, j // 4][:, :, col:col + P])
+            wd = work.tile([P, P // TG, P], F32, name="wide", align_bytes=64, bufs=NW)
+            col = (j % 2) * P
+            nc.vector.tensor_copy(out=wd[:], in_=raw_mm[i, j // 2][:, :, col:col + P])
             wide[i, j] = wd
 
-        def mix_chunk(i, j):
-            ps = bank("zt", [P, P // TG, TG * W])
-            for u in range(P // TG):
-                nc.tensor.matmul(ps[:, u, :], lhsT=wide[i, j][:, u, :],
-                                 rhs=diag[i][:, u * G + j // 2, :, :].rearrange("p t w -> p (t w)"), start=True, stop=True)
-            mm_banks[i, j] = ps
+        def mix_part(n):
+            i, j, part = n // 32, n % 32 // 4, n % 4
+            if part == 0:
+                mm_banks[i, j] = bank("zt", [P, P // TG, TG * W])
+                if j == 0:
+                    zt_mm[i] = work.tile([P, W, D // P, P], F32, name="zt_mm")
+            for u in (2 * part, 2 * part + 1):
+                nc.tensor.matmul(mm_banks[i, j][:, u, :], lhsT=wide[i, j][:, u, :],
+                                 rhs=diag[i, j // 2][:, u, :, :].rearrange("p t w -> p (t w)"), start=True, stop=True)
 
         def empty_chunk(i, j):
             nc.scalar.copy(out=zt_mm[i][:, :, j, :], in_=mm_banks[i, j][:].rearrange("p u (t w) -> p w (u t)", w=W))
 
-        def products(i, w, g, n_vec):
+        def products(i, w, g, n_vec, q):
+            n_vec = n_vec + (DV if q % 2 == 0 and q > 12 else 0)
             for l in range(L):
                 pr = work.tile([P, C], F32, name="prod", bufs=NPROD)
                 col = (w * L + l) * G + g
@@ -219,14 +243,13 @@ def tile_muddmultiwaydensegate_kernel(tc, past, wa, bb, gz, wq, wk, wv_bytes, wv
                     nc.scalar.activation(out=pr[:], in_=src, func=ACT.Copy, scale=dw[i][:, col:col + 1])
                 prods[i, w, g, l] = pr
 
-        def add_layers(i, w, g):
-            if g % 2 == 0:
+        def add_layers(i, w, g, c):
+            if g % 2 == 0 and c == 0:
                 zt_banks[i, w, g // 2] = bank("zt", [P, 4, P])
             ps = zt_banks[i, w, g // 2]
-            for c in range(2):
-                for l in range(L):
-                    nc.tensor.matmul(ps[:, 2 * (g % 2) + c, :], lhsT=prods[i, w, g, l][:, c * P:(c + 1) * P], rhs=ident[:],
-                                     is_transpose=True, start=(l == 0), stop=(l == L - 1))
+            for l in range(L):
+                nc.tensor.matmul(ps[:, 2 * (g % 2) + c, :], lhsT=prods[i, w, g, l][:, c * P:(c + 1) * P], rhs=ident[:],
+                                 is_transpose=True, start=(l == 0), stop=(l == L - 1))
 
         def empty_sums(i, w, h):
             sb = work.tile([P, 4, P], F32, name="zt_el", bufs=3)
@@ -353,15 +376,22 @@ def tile_muddmultiwaydensegate_kernel(tc, past, wa, bb, gz, wq, wk, wv_bytes, wv
         def stage_residual(i):
             for c in range(2):
                 cols = slice(c * HALF, (c + 1) * HALF)
-                z3 = z_banks[i, W - 1, c] if i < N_MM else acc[i][:, cols]
+                z3 = z_banks[i, W - 1, c] if (i, W - 1, c) in z_banks else acc[i][:, cols]
                 nc.vector.tensor_tensor(out=mixed[i][:, cols], in0=z3, in1=mixed[i][:, cols], op=ALU.add)
 
         depth_turn(first)
         depth_copy(first)
         depth_matmul(first)
+        for s in range(HD):
+            load_weight(0, s // 2, s % 2)
+        for l in range(L - 1):
+            load_x(first, l)
+        load_x(0, L - 1)
+        for s in range(HD, 3):
+            load_weight(0, s // 2, s % 2)
+        for s in range(HD):
+            interleave_weight(0, s // 2, s % 2)
         depth_bias(first)
-        load_weight(0, 0)
-        load_weight(0, 1)
         gain = []
         for w in range(3):
             gw = keep.tile([P, D], BF16, name="gain_%d" % w)
@@ -371,40 +401,54 @@ def tile_muddmultiwaydensegate_kernel(tc, past, wa, bb, gz, wq, wk, wv_bytes, wv
         nc.sync.dma_start(out=scale_sb[:], in_=wv_scale.rearrange("(h p j) o -> p h (j o)", h=2, j=4))
         neg_scale = keep.tile([P, 8], F32, name="neg_scale")
 
+        last = N_MM + N_EL - 1
+        rounds = [(N_MM + r // 3, r % 3) for r in range(3 * N_EL)] + ([(last, 3)] if TL else [])
+        n_mix = 4 * len(rounds)
+        n_parts = 32 * N_MM
+        span = 2 * (PE - P0)
+        parts = {}
+        for n in range(n_parts):
+            parts.setdefault(2 * P0 + n * span // n_parts, []).append(n)
+        first_q = {n // 4: s // 2 for s in sorted(parts, reverse=True) for n in parts[s] if n % 4 == 0}
+        last_q = {n // 4: s // 2 for s in sorted(parts) for n in parts[s] if n % 4 == 3}
         items = {}
         for r in range(3 * N_EL):
             items[4 * r + EB] = (N_MM + r // 3, r % 3)
-        for r in range(3 * N_MM):
-            items[4 * r + MB] = (r // 3, r % 3)
-        n_mix = 4 * 3 * N_EL
-        starts = (M0, M1, MB + 12, MB + 24)
-        chunks = {}
         for i in range(N_MM):
-            for j in range(8):
-                chunks[starts[i] + j * (starts[i + 1] - starts[i]) // 8] = (i, j)
-        depth = {12 * i + 3: i for i in range(N_MM)}
+            base = last_q[8 * i + 7] + 1
+            base += (EB + 2 - base) % 4
+            for w in range(3):
+                items[base + 4 * w] = (i, w)
+        depth = {1: 0, 11: 1, 25: 2}
         for k in range(1, N_EL):
             depth[12 * k - 5] = N_MM + k
-        for q in range(n_mix + EB + 6):
+        for q in range(max(items) + 9):
             r, g = divmod(q, 4)
             k, w = divmod(r, 3)
             tq = q % 12
             el = N_MM + k
-            if q < n_mix and tq == 2 and k + 1 < N_EL:
+            if q - RG in depth and depth[q - RG] < N_MM:
+                regroup_weights(depth[q - RG])
+            if q - RG - 1 in depth and depth[q - RG - 1] < N_MM:
+                fetch_weights(depth[q - RG - 1])
+            if q - SD in stores:
+                store(stores[q - SD])
+            if tq == 2 and k + 1 < N_EL:
                 load_x(el + 1, L - 1)
-            if q < n_mix and tq == 3 and k + 1 < N_EL:
+            if tq == LX and k + 1 < N_EL:
                 for l in range(L - 1):
                     load_x(el + 1, l)
-            if q in (3, 5):
-                load_weight(1, (q - 3) // 2)
-            if q in (6, 10):
-                load_weight(2, (q - 6) // 4)
-            if q + 2 in depth and depth[q + 2] < N_MM:
+            if 2 <= q <= 6:
+                s = q + 1
+                load_weight(s // 4, s % 4 // 2, s % 2)
+            if q in (6, 7):
+                load_wv(q - 6)
+            if q + 2 in depth and 0 < depth[q + 2] < N_MM:
                 load_x(depth[q + 2], L - 1)
-            if q + LM in starts[:N_MM]:
-                load_mm(starts.index(q + LM), 0)
-            if q + LM - 4 in starts[:N_MM]:
-                load_mm(starts.index(q + LM - 4), 1)
+            for ch in range(0, 8 * N_MM, 2):
+                if max(first_q[ch] - LM, 3) == q:
+                    load_mm(ch // 8, ch % 8 // 2)
+
             def at(name, fn):
                 off, ph = PLANS[PLAN][name]
                 if ph == phase and q - off in items:
@@ -414,8 +458,13 @@ def tile_muddmultiwaydensegate_kernel(tc, past, wa, bb, gz, wq, wk, wv_bytes, wv
                 if w == 2 and i < N_MM:
                     stage_back_residual(i)
 
+            def resid_last(i, w):
+                if w == 2 and TL and i == last:
+                    stage_back_residual(i)
+                    stage_residual(i)
+
             def resid(i, w):
-                if w == 2:
+                if w == 2 and not (TL and i == last):
                     stage_residual(i)
 
             def stages():
@@ -429,58 +478,62 @@ def tile_muddmultiwaydensegate_kernel(tc, past, wa, bb, gz, wq, wk, wv_bytes, wv
                 at("rback", resid_back)
                 at("resid", resid)
                 at("proj", stage_project)
+                at("rlast", resid_last)
                 at("sq", stage_squares)
                 at("rstd2", stage_rstd)
 
-            if q - SD in stores:
-                store(stores[q - SD])
             phase = "A"
-            if 1 <= q <= n_mix:
-                pr, pg = divmod(q - 1, 4)
-                add_layers(N_MM + pr // 3, pr % 3, pg)
+            for c in range(2):
+                if 1 <= q <= n_mix:
+                    pr, pg = divmod(q - 1, 4)
+                    add_layers(*rounds[pr], pg, c)
+                if c == 0:
+                    for n in parts.get(2 * q, []):
+                        mix_part(n)
             stages()
             if q == 6:
                 nc.vector.tensor_scalar(out=neg_scale[:], in0=scale_sb[:].rearrange("p h j -> p (h j)"), scalar1=-1.0,
                                         scalar2=None, op0=ALU.mult)
             if q < n_mix:
-                products(el, w, g, VH if q < 1 else VA if q < 13 else VB if q < MB else VC if q < MB + 24 else VD)
+                products(*rounds[r], g, VH if q < 1 else VT if q >= 60 else VA if q < 13 else VB if q < 23 else VC if q < PE else VD, q)
             phase = "B"
-            if q - 1 in chunks:
-                empty_chunk(*chunks[q - 1])
+            for ch in range(8 * N_MM):
+                if last_q[ch] == q - 1:
+                    empty_chunk(ch // 8, ch % 8)
             stages()
             if q - 1 in depth:
                 depth_copy(depth[q - 1])
             if q - 3 in depth:
                 depth_bias(depth[q - 3])
-                if depth[q - 3] < N_MM:
-                    regroup_weights(depth[q - 3])
             if 2 <= q <= n_mix and q % 2 == 0:
                 pr, pg = divmod(q - 1, 4)
-                empty_sums(N_MM + pr // 3, pr % 3, pg // 2)
+                empty_sums(*rounds[pr], pg // 2)
             phase = "C"
+            for n in parts.get(2 * q + 1, []):
+                mix_part(n)
             stages()
             if q in depth:
                 depth_turn(depth[q])
             if q - 2 in depth:
                 depth_matmul(depth[q - 2])
-            if q in chunks:
-                mix_chunk(*chunks[q])
             phase = "D"
             stages()
-            if q < n_mix:
-                for s in range(32 * tq // 12, 32 * (tq + 1) // 12):
+            if q < 60 and not (TL and el == last):
+                cum = lambda t: 32 * (CE * ((t + 1) // 2) + (6 - CE) * (t // 2)) // 36
+                for s in range(cum(tq), cum(tq + 1)):
                     chain(el, s // G, s % G)
             phase = "E"
             stages()
             if 2 <= q <= 13:
                 s = q - 2
                 quantize_weight(s // 4, s % 4 // 2, s % 2)
-            if 1 <= q <= 12:
+            if 1 + HD <= q <= 12:
                 s = q - 1
                 interleave_weight(s // 4, s % 4 // 2, s % 2)
             if 8 <= q <= 11:
                 widen_wv((q - 8) // 2, q % 2)
-            if q + WD in chunks:
-                widen_chunk(*chunks[q + WD])
-            if q + 1 in starts[:N_MM]:
-                build_diag(starts.index(q + 1))
+            for ch in range(8 * N_MM):
+                if first_q[ch] - WD == q:
+                    widen_chunk(ch // 8, ch % 8)
+                if ch % 2 == 0 and first_q[ch] - BD == q:
+                    build_diag(ch // 8, ch % 8 // 2)

@@ -22,67 +22,20 @@ AX = mybir.AxisListType
 
 P = 128
 HALF = 512
-N_MM = 3
-N_EL = 5
-TG = 16
-V_LAYERS = 3
-MANUAL = True
-ZT = 2
-ZB = 3
-NPROD = 20
-EB = 5
-MB = 25
-V0 = 3
-V1 = 3
-VH = 5
-MSG = 0
-PLAN = 4
-M0 = 12
-M1 = 24
-VA = 2
-VB = 3
-VC = 2
-VD = 3
-SD = 1
-WD = 2
-LM = 4
-P0 = 10
-PE = 50
-LX = 4
-TL = 0
-VT = 0
-RL = 4
-CE = 3
-DV = 1
-CH = 0
-CL = 12
-HD = 0
-NW = 5
-BD = 2
-RG = 4
-ONE = 1
+CHUNKS = D // P
+N_MM, N_PR = 3, 5
+TOK = P // L
+SETS = P // TOK
+RESID = W - 1
 
-X = (0, "-")
-PLANS = [
-    dict(back=(0, "C"), sq=(1, "B"), rstd=X, rstd2=(1, "B"), norm=(2, "E"), turn=(3, "C"), group=(4, "A"), quant=(4, "E"),
-         proj=(5, "C"), mix=(6, "A"), rback=(4, "C"), resid=(5, "B"), rlast=(RL, "D")),
-    dict(back=(0, "C"), sq=(1, "B"), rstd=(2, "A"), rstd2=X, norm=(2, "E"), turn=(3, "C"), group=(4, "A"), quant=(4, "E"),
-         proj=(5, "C"), mix=(6, "A"), rback=(4, "C"), resid=(5, "B"), rlast=(RL, "D")),
-    dict(back=(0, "C"), sq=(1, "A"), rstd=(1, "E"), rstd2=X, norm=(2, "B"), turn=(3, "C"), group=(4, "A"), quant=(4, "E"),
-         proj=(5, "C"), mix=(6, "A"), rback=(4, "C"), resid=(5, "B"), rlast=(RL, "D")),
-    dict(back=(0, "C"), sq=(1, "A"), rstd=(1, "E"), rstd2=X, norm=(2, "B"), turn=(2, "D"), group=(3, "B"), quant=(4, "A"),
-         proj=(4, "C"), mix=(5, "E"), rback=(3, "C"), resid=(4, "B"), rlast=(RL, "D")),
-    dict(back=(0, "C"), sq=(1, "A"), rstd=(2, "A"), rstd2=X, norm=(2, "E"), turn=(3, "C"), group=(4, "A"), quant=(4, "E"),
-         proj=(5, "C"), mix=(6, "A"), rback=(4, "C"), resid=(5, "B"), rlast=(RL, "D")),
-    dict(back=(0, "C"), sq=(1, "A"), rstd=(2, "A"), rstd2=X, norm=(2, "D"), turn=(3, "C"), group=(4, "A"), quant=(4, "E"),
-         proj=(5, "C"), mix=(6, "A"), rback=(4, "C"), resid=(5, "B"), rlast=(RL, "D")),
-    dict(back=(0, "C"), sq=(1, "A"), rstd=(1, "E"), rstd2=X, norm=(2, "B"), turn=(2, "D"), group=(3, "A"), quant=(3, "E"),
-         proj=(4, "C"), mix=(5, "E"), rback=(4, "C"), resid=(5, "B"), rlast=(RL, "D")),
-    dict(back=(0, "C"), sq=(1, "A"), rstd=(1, "E"), rstd2=X, norm=(2, "E"), turn=(3, "C"), group=(4, "A"), quant=(4, "B"),
-         proj=(4, "D"), mix=(5, "E"), rback=(4, "C"), resid=(5, "B"), rlast=(RL, "D")),
-    dict(back=(0, "C"), sq=(1, "A"), rstd=(2, "B"), rstd2=X, norm=(2, "E"), turn=(3, "C"), group=(4, "A"), quant=(4, "E"),
-         proj=(5, "C"), mix=(6, "B"), rback=(4, "C"), resid=(5, "B"), rlast=(RL, "D")),
-]
+VEC_LAYERS_FIRST, VEC_LAYERS_WEIGHTS, VEC_LAYERS = 5, 1, 2
+WEIGHT_STEPS = 18
+MM_STEPS = (10, 18, 34, 50)
+
+SQUARES, NORM, TURN, GROUP, PROJECT, COMBINE = 1, 2, 3, 4, 5, 6
+ROUND_TO_ITEM = 5
+LAST_STATE_LEAD, STATES_LEAD, DEPTH_LEAD, DEPTH_LEAD_MM = 8, 6, 5, 9
+WEIGHT_LEAD, BYTES_LEAD, SETS_LEAD, WIDEN_LEAD = 2, 4, 4, 2
 
 
 def tile_muddmultiwaydensegate_kernel(tc, past, wa, bb, gz, wq, wk, wv_bytes, wv_scale, out):
@@ -93,150 +46,139 @@ def tile_muddmultiwaydensegate_kernel(tc, past, wa, bb, gz, wq, wk, wv_bytes, wv
     with ExitStack() as ctx:
         keep = ctx.enter_context(tc.tile_pool(name="keep", bufs=1))
         work = ctx.enter_context(tc.tile_pool(name="work", bufs=2))
-        psum = ctx.enter_context(tc.psum_pool(name="psum", bufs=1))
-        if MANUAL:
-            ctx.enter_context(tc.manual_schedule())
+        psum = ctx.enter_context(tc.psum_pool(name="psum", bufs=8))
+        ctx.enter_context(tc.manual_schedule())
 
-        def bank(tag, shape, dtype=F32):
-            if ONE:
-                return psum.tile(shape, dtype, name=tag, tag="bank", bufs=8)
-            return psum.tile(shape, dtype, name=tag, tag=tag, bufs={"zt": ZT, "z": ZB, "misc": 8 - ZT - ZB}[tag])
+        def bank(shape, dtype=F32):
+            return psum.tile(shape, dtype, name="bank")
 
-        mm_banks, nt_banks, proj, step1, wv_planes, stores = {}, {}, {}, {}, {}, {}
-        x_tiles, dw, coef, diag, zt_mm, raw_mm = {}, {}, {}, {}, {}, {}
-        prods, zt_banks, zt_sb, z_banks, rstd, n_perm, n_grp, n_mx = {}, {}, {}, {}, {}, {}, {}, {}
-        gate, mixed, acc, w_raw, w_grp, w_mx, wide, ssq = {}, {}, {}, {}, {}, {}, {}, {}
+        def copy_out(on_vector, dst, src):
+            if on_vector:
+                nc.vector.tensor_copy(out=dst, in_=src)
+            else:
+                nc.scalar.copy(out=dst, in_=src)
 
-        def load_x(i, l):
-            x = work.tile([P, D], BF16, name="x", bufs=18)
+        def half(c):
+            return slice(c * HALF, (c + 1) * HALF)
+
+        states, depth_part, dw = {}, {}, {}
+        w_raw, wv_raw, w_grouped, w_mx = {}, {}, {}, {}
+        coef, diag, set_raw, set_wide, mm_bank, zt_mm = {}, {}, {}, {}, {}, {}
+        prods, sum_bank, zt_pr, chain_acc = {}, {}, {}, {}
+        z_bank, sq_sum, rstd, n_words, nt_bank, n_grouped, n_mx, proj_bank, term = {}, {}, {}, {}, {}, {}, {}, {}, {}
+
+        def load_state(i, l):
+            x = work.tile([P, D], BF16, name="state", bufs=2 * L + 2)
             nc.sync.dma_start(out=x[:], in_=xs[l, i * P:(i + 1) * P, :])
-            x_tiles[i, l] = x
-
-        first = N_MM
-        load_x(first, L - 1)
-        wa_sb = keep.tile([P, D // P, M], BF16, name="wa_sb")
-        nc.sync.dma_start(out=wa_sb[:], in_=wa.rearrange("(j p) m -> p j m", p=P))
-        bias = keep.tile([P, M], BF16, name="bias")
-        nc.sync.dma_start(out=bias[:], in_=bb.partition_broadcast(P))
-        ident = keep.tile([P, P], F32, name="ident")
-        make_identity(nc, ident[:])
-        ident_bf = keep.tile([P, P], BF16, name="ident_bf")
-        nc.vector.tensor_copy(out=ident_bf[:], in_=ident[:])
-        own = keep.tile([P, TG], F32, name="own")
-        nc.vector.tensor_reduce(out=own[:], in_=ident[:].rearrange("p (t l) -> p t l", l=L), axis=AX.X, op=ALU.add)
-        minus_half = keep.tile([P, 1], F32, name="minus_half")
-        nc.gpsimd.memset(minus_half[:], -0.5)
+            states[i, l] = x
 
         def load_weight(w, h, c):
             raw = work.tile([P, 4, HALF], BF16, name="raw", bufs=4)
-            src = (wq, wk)[w][h * HALF:(h + 1) * HALF, c * HALF:(c + 1) * HALF]
-            nc.sync.dma_start(out=raw[:], in_=src.rearrange("(p j) n -> p j n", j=4))
+            nc.sync.dma_start(out=raw[:], in_=(wq, wk)[w][half(h), half(c)].rearrange("(p j) n -> p j n", j=4))
             w_raw[w, h, c] = raw
 
         def load_wv(h):
-            raw = work.tile([P, 4 * D], U8, name="wv_codes", bufs=2)
-            nc.sync.dma_start(out=raw[:], in_=wv_bytes[h * HALF:(h + 1) * HALF, :].rearrange("(p j) n -> p (j n)", j=4))
-            w_raw[2, h] = raw
+            codes_in = work.tile([P, 4 * D], U8, name="wv_in")
+            nc.sync.dma_start(out=codes_in[:], in_=wv_bytes[half(h), :].rearrange("(p j) n -> p (j n)", j=4))
+            wv_raw[h] = codes_in
+
+        def load_sets(i, g):
+            raw = work.tile([P, SETS, C], BF16, name="raw", bufs=4)
+            for u in range(SETS):
+                tokens = slice(i * P + u * TOK, i * P + (u + 1) * TOK)
+                nc.sync.dma_start(out=raw[:, u, :], in_=xs[:, tokens, g * C:(g + 1) * C].rearrange("l t d -> t l d"))
+            set_raw[i, g] = raw
 
         def widen_wv(h, c):
-            planes = work.tile([P, 4, HALF], BF16, name="wide", align_bytes=64, bufs=NW)
+            planes = work.tile([P, 4, HALF], BF16, name="stage", align_bytes=64, bufs=4)
             for j in range(4):
                 col = j * D + c * HALF
-                nc.scalar.activation(out=planes[:, j, :], in_=w_raw[2, h][:, col:col + HALF].bitcast(FP8),
+                nc.scalar.activation(out=planes[:, j, :], in_=wv_raw[h][:, col:col + HALF].bitcast(FP8),
                                      func=ACT.Copy, scale=neg_scale[:, 4 * h + j:4 * h + j + 1])
-            wv_planes[h, c] = planes
+            w_raw[2, h, c] = planes
 
         def interleave_weight(w, h, c):
-            grp = work.tile([P, HALF, 4], BF16, name="wide", align_bytes=64, bufs=NW)
-            src = w_raw[w, h, c][:] if w < 2 else wv_planes[h, c][:]
-            nc.vector.tensor_copy(out=grp[:].rearrange("p (c i) j -> p c j i", i=4),
-                                  in_=src.rearrange("p j (c i) -> p c j i", i=4))
-            w_grp[w, h, c] = grp
+            grouped = work.tile([P, HALF, 4], BF16, name="stage", align_bytes=64, bufs=4)
+            nc.vector.tensor_copy(out=grouped[:].rearrange("p (n i) j -> p n j i", i=4),
+                                  in_=w_raw[w, h, c][:].rearrange("p j (n i) -> p n j i", i=4))
+            w_grouped[w, h, c] = grouped
 
         def quantize_weight(w, h, c):
             codes = keep.tile([P, HALF], U32, name="w_codes_%d%d%d" % (w, h, c), align_bytes=64)
             scales = keep.tile([P, HALF], U8, name="w_scales_%d%d%d" % (w, h, c), align_bytes=64)
             nc.vector.quantize_mx(out=codes[:].bitcast(FP8X4), scales=scales[:],
-                                  in_=w_grp[w, h, c][:].rearrange("p c j -> p (c j)"))
+                                  in_=w_grouped[w, h, c][:].rearrange("p n j -> p (n j)"))
             w_mx[w, h, c] = (codes, scales)
 
         def depth_turn(i):
-            xt_ps = bank("misc", [P, D // P, P], BF16)
-            for j in range(D // P):
-                nc.tensor.transpose(xt_ps[:, j, :], x_tiles[i, L - 1][:, j * P:(j + 1) * P], ident_bf[:])
-            step1[i] = xt_ps
+            ps = bank([P, CHUNKS, P], BF16)
+            for j in range(CHUNKS):
+                nc.tensor.transpose(ps[:, j, :], states[i, L - 1][:, j * P:(j + 1) * P], ident_bf[:])
+            depth_part[i] = ps
 
         def depth_copy(i):
-            xt = work.tile([P, D // P, P], BF16, name="xt", bufs=1)
-            nc.scalar.copy(out=xt[:], in_=step1[i][:])
-            step1[i] = xt
+            last_t = work.tile([P, CHUNKS, P], BF16, name="last_t", bufs=1)
+            nc.scalar.copy(out=last_t[:], in_=depth_part[i][:])
+            depth_part[i] = last_t
 
         def depth_matmul(i):
-            dw_ps = bank("misc", [P, M])
-            for j in range(D // P):
-                nc.tensor.matmul(dw_ps[:], lhsT=step1[i][:, j, :], rhs=wa_sb[:, j, :], start=(j == 0), stop=(j == D // P - 1))
-            step1[i] = dw_ps
+            ps = bank([P, M])
+            for j in range(CHUNKS):
+                nc.tensor.matmul(ps[:], lhsT=depth_part[i][:, j, :], rhs=wa_sb[:, j, :],
+                                 start=(j == 0), stop=(j == CHUNKS - 1))
+            depth_part[i] = ps
 
         def depth_bias(i):
-            dw_ps = step1[i]
             d = work.tile([P, M], F32, name="dw", bufs=3)
             if i >= N_MM:
-                nc.vector.tensor_tensor(out=d[:], in0=dw_ps[:], in1=bias[:], op=ALU.add)
+                nc.vector.tensor_tensor(out=d[:], in0=depth_part[i][:], in1=bias[:], op=ALU.add)
             else:
                 nc.vector.tensor_tensor(out=d[:].rearrange("p (s w) -> p s w", w=W),
-                                        in0=dw_ps[:].rearrange("p (w s) -> p s w", w=W),
+                                        in0=depth_part[i][:].rearrange("p (w s) -> p s w", w=W),
                                         in1=bias[:].rearrange("p (w s) -> p s w", w=W), op=ALU.add)
             dw[i] = d
 
-        def regroup_weights(i):
-            park = rows[i * P:i * P + P * M // D, :].rearrange("a (b m) -> (a b) m", m=M)
-            nc.sync.dma_start(out=park, in_=dw[i][:])
+        def parking(i):
+            return rows[i * P:i * P + P * M // D, :].rearrange("a (b m) -> (a b) m", m=M)
+
+        def park_weights(i):
+            nc.sync.dma_start(out=parking(i), in_=dw[i][:])
 
         def fetch_weights(i):
-            park = rows[i * P:i * P + P * M // D, :].rearrange("a (b m) -> (a b) m", m=M)
-            cf = work.tile([P, P // TG, G * W], F32, name="coef")
-            nc.sync.dma_start(out=cf[:], in_=park.rearrange("(u t) (l x) -> (t l) u x", t=TG, l=L))
+            cf = work.tile([P, SETS, G * W], F32, name="coef")
+            nc.sync.dma_start(out=cf[:], in_=parking(i).rearrange("(u t) (l x) -> (t l) u x", t=TOK, l=L))
             coef[i] = cf
 
         def build_diag(i, g):
-            dg = work.tile([P, P // TG, TG, W], F32, name="diag")
-            shape = [P, P // TG, TG, W]
+            shape = [P, SETS, TOK, W]
+            dg = work.tile(shape, F32, name="diag")
             nc.vector.tensor_tensor(out=dg[:], in0=coef[i][:, :, g * W:(g + 1) * W].unsqueeze(2).to_broadcast(shape),
-                                    in1=own[:].unsqueeze(1).unsqueeze(3).to_broadcast(shape), op=ALU.mult)
+                                    in1=own_token[:].unsqueeze(1).unsqueeze(3).to_broadcast(shape), op=ALU.mult)
             diag[i, g] = dg
 
-        def load_mm(i, g):
-            raw = work.tile([P, P // TG, C], BF16, name="raw", bufs=4)
-            for u in range(P // TG):
-                tok = slice(i * P + u * TG, i * P + (u + 1) * TG)
-                nc.sync.dma_start(out=raw[:, u, :], in_=xs[:, tok, g * C:(g + 1) * C].rearrange("l t d -> t l d"))
-            raw_mm[i, g] = raw
-
         def widen_chunk(i, j):
-            wd = work.tile([P, P // TG, P], F32, name="wide", align_bytes=64, bufs=NW)
+            wide = work.tile([P, SETS, P], F32, name="stage", align_bytes=64, bufs=4)
             col = (j % 2) * P
-            nc.vector.tensor_copy(out=wd[:], in_=raw_mm[i, j // 2][:, :, col:col + P])
-            wide[i, j] = wd
+            nc.vector.tensor_copy(out=wide[:], in_=set_raw[i, j // 2][:, :, col:col + P])
+            set_wide[i, j] = wide
 
-        def mix_part(n):
-            i, j, part = n // 32, n % 32 // 4, n % 4
+        def mix_sets(i, j, part):
             if part == 0:
-                mm_banks[i, j] = bank("zt", [P, P // TG, TG * W])
+                mm_bank[i, j] = bank([P, SETS, TOK * W])
                 if j == 0:
-                    zt_mm[i] = work.tile([P, W, D // P, P], F32, name="zt_mm")
-            for u in (2 * part, 2 * part + 1):
-                nc.tensor.matmul(mm_banks[i, j][:, u, :], lhsT=wide[i, j][:, u, :],
+                    zt_mm[i] = work.tile([P, W, CHUNKS, P], F32, name="zt_mm")
+            for u in range(part * SETS // 2, (part + 1) * SETS // 2):
+                nc.tensor.matmul(mm_bank[i, j][:, u, :], lhsT=set_wide[i, j][:, u, :],
                                  rhs=diag[i, j // 2][:, u, :, :].rearrange("p t w -> p (t w)"), start=True, stop=True)
 
         def empty_chunk(i, j):
-            nc.scalar.copy(out=zt_mm[i][:, :, j, :], in_=mm_banks[i, j][:].rearrange("p u (t w) -> p w (u t)", w=W))
+            nc.scalar.copy(out=zt_mm[i][:, :, j, :], in_=mm_bank[i, j][:].rearrange("p u (t w) -> p w (u t)", w=W))
 
-        def products(i, w, g, n_vec, q):
-            n_vec = n_vec + (DV if q % 2 == 0 and q > 12 else 0)
+        def products(i, w, g, n_vec):
             for l in range(L):
-                pr = work.tile([P, C], F32, name="prod", bufs=NPROD)
+                pr = work.tile([P, C], F32, name="prod", bufs=20)
                 col = (w * L + l) * G + g
-                src = x_tiles[i, l][:, g * C:(g + 1) * C]
+                src = states[i, l][:, g * C:(g + 1) * C]
                 if l < n_vec:
                     nc.vector.tensor_scalar(out=pr[:], in0=src, scalar1=dw[i][:, col:col + 1], scalar2=None, op0=ALU.mult)
                 else:
@@ -245,295 +187,288 @@ def tile_muddmultiwaydensegate_kernel(tc, past, wa, bb, gz, wq, wk, wv_bytes, wv
 
         def add_layers(i, w, g, c):
             if g % 2 == 0 and c == 0:
-                zt_banks[i, w, g // 2] = bank("zt", [P, 4, P])
-            ps = zt_banks[i, w, g // 2]
+                sum_bank[i, w, g // 2] = bank([P, 4, P])
             for l in range(L):
-                nc.tensor.matmul(ps[:, 2 * (g % 2) + c, :], lhsT=prods[i, w, g, l][:, c * P:(c + 1) * P], rhs=ident[:],
-                                 is_transpose=True, start=(l == 0), stop=(l == L - 1))
+                nc.tensor.matmul(sum_bank[i, w, g // 2][:, 2 * (g % 2) + c, :], lhsT=prods[i, w, g, l][:, c * P:(c + 1) * P],
+                                 rhs=ident[:], is_transpose=True, start=(l == 0), stop=(l == L - 1))
 
-        def empty_sums(i, w, h):
-            sb = work.tile([P, 4, P], F32, name="zt_el", bufs=3)
-            nc.scalar.copy(out=sb[:], in_=zt_banks[i, w, h][:])
-            zt_sb[i, w, h] = sb
+        def empty_sums(i, w, h, on_vector):
+            zt = work.tile([P, 4, P], F32, name="zt_pr", bufs=3)
+            copy_out(on_vector, zt[:], sum_bank[i, w, h][:])
+            zt_pr[i, w, h] = zt
 
         def chain(i, l, g):
             if l == 0 and g == 0:
-                acc[i] = work.tile([P, D], F32, name="acc")
-            col = ((W - 1) * L + l) * G + g
+                chain_acc[i] = work.tile([P, D], F32, name="chain_acc")
+            col = (RESID * L + l) * G + g
             cols = slice(g * C, (g + 1) * C)
             if l == 0:
-                nc.vector.tensor_scalar(out=acc[i][:, cols], in0=x_tiles[i, l][:, cols], scalar1=dw[i][:, col:col + 1],
-                                        scalar2=None, op0=ALU.mult)
+                nc.vector.tensor_scalar(out=chain_acc[i][:, cols], in0=states[i, l][:, cols],
+                                        scalar1=dw[i][:, col:col + 1], scalar2=None, op0=ALU.mult)
             else:
-                nc.vector.scalar_tensor_tensor(out=acc[i][:, cols], in0=x_tiles[i, l][:, cols], scalar=dw[i][:, col:col + 1],
-                                               in1=acc[i][:, cols], op0=ALU.mult, op1=ALU.add)
+                nc.vector.scalar_tensor_tensor(out=chain_acc[i][:, cols], in0=states[i, l][:, cols],
+                                               scalar=dw[i][:, col:col + 1], in1=chain_acc[i][:, cols],
+                                               op0=ALU.mult, op1=ALU.add)
 
-        def turn_back(i, w, h, tag):
-            ps = bank(tag, [P, 4, P])
-            for c in range(4):
-                src = zt_mm[i][:, w, 4 * h + c, :] if i < N_MM else zt_sb[i, w, h][:, c, :]
-                nc.tensor.transpose(ps[:, c, :], src, ident[:])
-            return ps[:].rearrange("p c k -> p (c k)")
-
-        def stage_back(i, w):
+        def turn_back(i, w):
             for h in range(2):
-                z_banks[i, w, h] = turn_back(i, w, h, "z")
+                ps = bank([P, 4, P])
+                for c in range(4):
+                    src = zt_mm[i][:, w, 4 * h + c, :] if i < N_MM else zt_pr[i, w, h][:, c, :]
+                    nc.tensor.transpose(ps[:, c, :], src, ident[:])
+                z_bank[i, w, h] = ps[:].rearrange("t c k -> t (c k)")
 
-        def stage_squares(i, w):
-            ss = work.tile([P, 2], F32, name="ss", bufs=3)
+        def squares(i, w):
+            ss = work.tile([P, 2], F32, name="sq_sum", bufs=3)
             for h in range(2):
-                junk = work.tile([P, HALF], BF16, name="squares")
-                nc.scalar.activation(out=junk[:], in_=z_banks[i, w, h], func=ACT.Square, scale=D ** -0.5,
+                sq = work.tile([P, HALF], BF16, name="sq")
+                nc.scalar.activation(out=sq[:], in_=z_bank[i, w, h], func=ACT.Square, scale=D ** -0.5,
                                      accum_out=ss[:, h:h + 1])
-            ssq[i, w] = ss
+            sq_sum[i, w] = ss
 
-        def stage_rstd(i, w):
+        def inverse_root(i, w):
             ms = work.tile([P, 1], F32, name="ms", bufs=3)
-            (nc.gpsimd if MSG else nc.vector).tensor_scalar(out=ms[:], in0=ssq[i, w][:, 0:1], scalar1=ssq[i, w][:, 1:2], scalar2=EPS,
+            nc.vector.tensor_scalar(out=ms[:], in0=sq_sum[i, w][:, 0:1], scalar1=sq_sum[i, w][:, 1:2], scalar2=EPS,
                                     op0=ALU.add, op1=ALU.add)
             r = work.tile([P, 1], F32, name="rstd", bufs=3)
             nc.gpsimd.tensor_tensor(out=r[:], in0=ms[:], in1=minus_half[:], op=ALU.pow)
             rstd[i, w] = r
 
-        def stage_norm(i, w):
-            n = work.tile([P, 2, 2, P, 2], BF16, name="n_perm")
+        def norm(i, w):
+            n = work.tile([P, 2, 2, P, 2], BF16, name="n_words")
             for h in range(2):
                 for u in range(2):
                     nc.vector.scalar_tensor_tensor(
                         out=n[:, h, u, :, :],
-                        in0=z_banks[i, w, h].rearrange("t (p u e) -> t u p e", u=2, e=2)[:, u, :, :],
+                        in0=z_bank[i, w, h].rearrange("t (p u e) -> t u p e", u=2, e=2)[:, u, :, :],
                         scalar=rstd[i, w][:],
-                        in1=gain[w][:, h * HALF:(h + 1) * HALF].rearrange("t (p u e) -> t u p e", u=2, e=2)[:, u, :, :],
+                        in1=gain[w][:, half(h)].rearrange("t (p u e) -> t u p e", u=2, e=2)[:, u, :, :],
                         op0=ALU.mult, op1=ALU.mult)
-            n_perm[i, w] = n
+            n_words[i, w] = n
 
-        def stage_turn(i, w):
-            words = n_perm[i, w][:].rearrange("t h u p e -> t (h u p e)").bitcast(F32)
-            ps = bank("misc", [P, 2, 2, P])
+        def turn(i, w):
+            words = n_words[i, w][:].rearrange("t h u p e -> t (h u p e)").bitcast(F32)
+            ps = bank([P, 2, 2, P])
             for h in range(2):
                 for u in range(2):
                     s = 2 * h + u
                     nc.tensor.transpose(ps[:, h, u, :], words[:, s * P:(s + 1) * P], ident[:])
-            nt_banks[i, w] = ps
+            nt_bank[i, w] = ps
 
-        def stage_group(i, w):
-            ps = nt_banks[i, w]
-            grp = work.tile([P, D], BF16, name="n_grp", align_bytes=64)
-            nc.scalar.copy(out=grp[:].bitcast(F32).rearrange("p (h t u) -> p h t u", h=2, u=2),
-                           in_=ps[:].rearrange("p h u t -> p h t u"))
-            n_grp[i, w] = grp
+        def group(i, w, on_vector):
+            grouped = work.tile([P, D], BF16, name="n_grouped", align_bytes=64)
+            copy_out(on_vector, grouped[:].bitcast(F32).rearrange("p (h t u) -> p h t u", h=2, u=2),
+                     nt_bank[i, w][:].rearrange("p h u t -> p h t u"))
+            n_grouped[i, w] = grouped
 
-        def stage_quantize(i, w):
+        def quantize(i, w):
             codes = work.tile([P, 2 * P], U32, name="n_codes", align_bytes=64)
             scales = work.tile([P, 2 * P], U8, name="n_scales", align_bytes=64)
-            nc.vector.quantize_mx(out=codes[:].bitcast(FP8X4), scales=scales[:], in_=n_grp[i, w][:])
+            nc.vector.quantize_mx(out=codes[:].bitcast(FP8X4), scales=scales[:], in_=n_grouped[i, w][:])
             n_mx[i, w] = (codes, scales)
 
-        def stage_project(i, w):
+        def project(i, w):
             codes, scales = n_mx[i, w]
             for c in range(2):
-                ps = bank("misc", [P, HALF])
+                ps = bank([P, HALF])
                 for h in range(2):
                     nc.tensor.matmul_mx(out=ps[:], lhsT=codes[:, h * P:(h + 1) * P].bitcast(FP8X4),
                                         lhsT_scale=scales[:, h * P:(h + 1) * P],
                                         rhs=w_mx[w, h, c][0][:].bitcast(FP8X4), rhs_scale=w_mx[w, h, c][1][:],
                                         start=(h == 0), stop=(h == 1))
-                proj[i, w, c] = ps
+                proj_bank[i, w, c] = ps
 
-        def stage_mix(i, w):
-            if w == 0:
-                gate[i] = work.tile([P, D], F32, name="gate", bufs=3)
-            if w == 1:
-                mixed[i] = work.tile([P, D], F32, name="mixed", bufs=3)
-            res = []
+        def combine(i, w):
+            res = work.tile([P, D], F32, name=("gate", "key_term", "result")[w])
+            term[i, w] = res
             for c in range(2):
-                ps = proj[i, w, c]
-                cols = slice(c * HALF, (c + 1) * HALF)
+                ps = proj_bank[i, w, c][:]
                 if w == 0:
-                    nc.scalar.activation(out=gate[i][:, cols], in_=ps[:], func=ACT.Sigmoid)
+                    nc.scalar.activation(out=res[:, half(c)], in_=ps, func=ACT.Sigmoid)
                 elif w == 1:
-                    nc.vector.tensor_tensor(out=mixed[i][:, cols], in0=ps[:], in1=gate[i][:, cols], op=ALU.mult)
+                    nc.vector.tensor_tensor(out=res[:, half(c)], in0=ps, in1=term[i, 0][:, half(c)], op=ALU.mult)
                 else:
-                    b = work.tile([P, HALF], F32, name="rest")
-                    nc.vector.scalar_tensor_tensor(out=b[:], in0=gate[i][:, cols], scalar=1.0, in1=ps[:],
+                    nc.vector.scalar_tensor_tensor(out=res[:, half(c)], in0=term[i, 0][:, half(c)], scalar=1.0, in1=ps,
                                                    op0=ALU.subtract, op1=ALU.mult)
-                    res.append(b)
-            for c in range(len(res)):
-                cols = slice(c * HALF, (c + 1) * HALF)
-                nc.vector.tensor_tensor(out=mixed[i][:, cols], in0=mixed[i][:, cols], in1=res[c][:], op=ALU.add)
             if w == 2:
-                stores[q] = i
+                for c in range(2):
+                    nc.vector.tensor_tensor(out=res[:, half(c)], in0=res[:, half(c)], in1=term[i, 1][:, half(c)], op=ALU.add)
+
+        def add_residual(i):
+            for c in range(2):
+                z3 = z_bank[i, RESID, c] if i < N_MM else chain_acc[i][:, half(c)]
+                nc.vector.tensor_tensor(out=term[i, 1][:, half(c)], in0=z3, in1=term[i, 1][:, half(c)], op=ALU.add)
 
         def store(i):
             for c in range(2):
-                cols = slice(c * HALF, (c + 1) * HALF)
-                nc.sync.dma_start(out=rows[i * P:(i + 1) * P, cols], in_=mixed[i][:, cols])
+                nc.sync.dma_start(out=rows[i * P:(i + 1) * P, half(c)], in_=term[i, 2][:, half(c)])
 
-        def stage_back_residual(i):
-            for c in range(2):
-                z_banks[i, W - 1, c] = turn_back(i, W - 1, c, "misc")
+        first, second = N_MM, N_MM + 1
+        rounds = [(i, w) for i in range(N_MM, N_MM + N_PR) for w in range(3)]
+        rounds.remove((second, 0))
+        rounds.insert(1, (second, 0))
+        n_steps = G * len(rounds)
+        tile_step = {i: G * rounds.index((i, 0)) for i in range(N_MM, N_MM + N_PR)}
+        pieces = [(w, h, c) for w in range(3) for h in range(2) for c in range(2)]
+        pieces = pieces[8:10] + pieces[:8] + pieces[10:]
+        piece_step = [s * WEIGHT_STEPS // len(pieces) for s in range(len(pieces))]
+        mix_at, chunk_first, chunk_last = {}, {}, {}
+        for i in range(N_MM):
+            for n in range(2 * CHUNKS):
+                place = 2 * MM_STEPS[i] + n * (MM_STEPS[i + 1] - MM_STEPS[i]) // CHUNKS
+                mix_at[place] = (i, n // 2, n % 2)
+                chunk_first.setdefault((i, n // 2), place // 2)
+                chunk_last[i, n // 2] = place // 2
+        items = {G * r + ROUND_TO_ITEM: rounds[r] for r in range(len(rounds))}
+        for i in range(N_MM):
+            for w in range(3):
+                items[MM_STEPS[i + 1] + 1 + G * w] = (i, w)
+        depth = {max(tile_step[i] - DEPTH_LEAD, 0): i for i in range(second, N_MM + N_PR)}
+        for i in range(N_MM):
+            depth[max(MM_STEPS[i] - DEPTH_LEAD_MM, 2)] = i
 
-        def stage_residual(i):
-            for c in range(2):
-                cols = slice(c * HALF, (c + 1) * HALF)
-                z3 = z_banks[i, W - 1, c] if (i, W - 1, c) in z_banks else acc[i][:, cols]
-                nc.vector.tensor_tensor(out=mixed[i][:, cols], in0=z3, in1=mixed[i][:, cols], op=ALU.add)
+        def item(q, stage):
+            return items.get(q - stage)
 
+        def last_way(q, stage):
+            it = item(q, stage)
+            return it[0] if it is not None and it[1] == 2 else None
+
+        def needs_cover(q):
+            combining = item(q, COMBINE)
+            return item(q, NORM) is not None and (combining is None or combining[1] == 0)
+
+        load_state(first, L - 1)
+        wa_sb = keep.tile([P, CHUNKS, M], BF16, name="wa_sb")
+        nc.sync.dma_start(out=wa_sb[:], in_=wa.rearrange("(j p) m -> p j m", p=P))
+        bias = keep.tile([P, M], BF16, name="bias")
+        nc.sync.dma_start(out=bias[:], in_=bb.partition_broadcast(P))
+        scale_sb = keep.tile([P, 2, 4], F32, name="scale_sb")
+        nc.sync.dma_start(out=scale_sb[:], in_=wv_scale.rearrange("(h p j) o -> p h (j o)", h=2, j=4))
+        load_wv(0)
+        load_state(second, L - 1)
+        for l in range(L - 1):
+            load_state(first, l)
+        load_weight(*pieces[2])
+        load_state(0, L - 1)
+        load_weight(*pieces[3])
+        gain = []
+        for w in range(3):
+            gain_w = keep.tile([P, D], BF16, name="gain_%d" % w)
+            nc.sync.dma_start(out=gain_w[:], in_=gz[w, :].partition_broadcast(P))
+            gain.append(gain_w)
+
+        ident = keep.tile([P, P], F32, name="ident")
+        make_identity(nc, ident[:])
+        ident_bf = keep.tile([P, P], BF16, name="ident_bf")
+        nc.vector.tensor_copy(out=ident_bf[:], in_=ident[:])
+        own_token = keep.tile([P, TOK], F32, name="own_token")
+        nc.vector.tensor_reduce(out=own_token[:], in_=ident[:].rearrange("p (t l) -> p t l", l=L), axis=AX.X, op=ALU.add)
+        minus_half = keep.tile([P, 1], F32, name="minus_half")
+        nc.gpsimd.memset(minus_half[:], -0.5)
+        neg_scale = keep.tile([P, 8], F32, name="neg_scale")
+        nc.vector.tensor_scalar(out=neg_scale[:], in0=scale_sb[:].rearrange("p h j -> p (h j)"), scalar1=-1.0,
+                                scalar2=None, op0=ALU.mult)
         depth_turn(first)
         depth_copy(first)
         depth_matmul(first)
-        for s in range(HD):
-            load_weight(0, s // 2, s % 2)
-        for l in range(L - 1):
-            load_x(first, l)
-        load_x(0, L - 1)
-        for s in range(HD, 3):
-            load_weight(0, s // 2, s % 2)
-        for s in range(HD):
-            interleave_weight(0, s // 2, s % 2)
+        widen_wv(0, 0)
+        widen_wv(0, 1)
         depth_bias(first)
-        gain = []
-        for w in range(3):
-            gw = keep.tile([P, D], BF16, name="gain_%d" % w)
-            nc.sync.dma_start(out=gw[:], in_=gz[w, :].partition_broadcast(P))
-            gain.append(gw)
-        scale_sb = keep.tile([P, 2, 4], F32, name="scale_sb")
-        nc.sync.dma_start(out=scale_sb[:], in_=wv_scale.rearrange("(h p j) o -> p h (j o)", h=2, j=4))
-        neg_scale = keep.tile([P, 8], F32, name="neg_scale")
 
-        last = N_MM + N_EL - 1
-        rounds = [(N_MM + r // 3, r % 3) for r in range(3 * N_EL)] + ([(last, 3)] if TL else [])
-        n_mix = 4 * len(rounds)
-        n_parts = 32 * N_MM
-        span = 2 * (PE - P0)
-        parts = {}
-        for n in range(n_parts):
-            parts.setdefault(2 * P0 + n * span // n_parts, []).append(n)
-        first_q = {n // 4: s // 2 for s in sorted(parts, reverse=True) for n in parts[s] if n % 4 == 0}
-        last_q = {n // 4: s // 2 for s in sorted(parts) for n in parts[s] if n % 4 == 3}
-        items = {}
-        for r in range(3 * N_EL):
-            items[4 * r + EB] = (N_MM + r // 3, r % 3)
-        for i in range(N_MM):
-            base = last_q[8 * i + 7] + 1
-            base += (EB + 2 - base) % 4
-            for w in range(3):
-                items[base + 4 * w] = (i, w)
-        depth = {1: 0, 11: 1, 25: 2}
-        for k in range(1, N_EL):
-            depth[12 * k - 5] = N_MM + k
-        for q in range(max(items) + 9):
-            r, g = divmod(q, 4)
-            k, w = divmod(r, 3)
-            tq = q % 12
-            el = N_MM + k
-            if q - RG in depth and depth[q - RG] < N_MM:
-                regroup_weights(depth[q - RG])
-            if q - RG - 1 in depth and depth[q - RG - 1] < N_MM:
-                fetch_weights(depth[q - RG - 1])
-            if q - SD in stores:
-                store(stores[q - SD])
-            if tq == 2 and k + 1 < N_EL:
-                load_x(el + 1, L - 1)
-            if tq == LX and k + 1 < N_EL:
-                for l in range(L - 1):
-                    load_x(el + 1, l)
-            if 2 <= q <= 6:
-                s = q + 1
-                load_weight(s // 4, s % 4 // 2, s % 2)
-            if q in (6, 7):
-                load_wv(q - 6)
-            if q + 2 in depth and 0 < depth[q + 2] < N_MM:
-                load_x(depth[q + 2], L - 1)
-            for ch in range(0, 8 * N_MM, 2):
-                if max(first_q[ch] - LM, 3) == q:
-                    load_mm(ch // 8, ch % 8 // 2)
+        for q in range(max(items) + COMBINE + 2):
+            if depth.get(q - 4, N_MM) < N_MM:
+                park_weights(depth[q - 4])
+            if depth.get(q - 5, N_MM) < N_MM:
+                fetch_weights(depth[q - 5])
+            if last_way(q - 1, COMBINE) is not None:
+                store(last_way(q - 1, COMBINE))
+            for i in range(second, N_MM + N_PR):
+                if q == tile_step[i] - LAST_STATE_LEAD:
+                    load_state(i, L - 1)
+                if q == max(tile_step[i] - STATES_LEAD, 0):
+                    for l in range(L - 1):
+                        load_state(i, l)
+            for s in range(4, 10):
+                if q == piece_step[s] - WEIGHT_LEAD:
+                    load_weight(*pieces[s])
+            if q == piece_step[10] - BYTES_LEAD:
+                load_wv(1)
+            if 0 < depth.get(q + 2, 0) < N_MM:
+                load_state(depth[q + 2], L - 1)
+            for i in range(N_MM):
+                for g in range(G):
+                    if q == chunk_first[i, 2 * g] - SETS_LEAD:
+                        load_sets(i, g)
 
-            def at(name, fn):
-                off, ph = PLANS[PLAN][name]
-                if ph == phase and q - off in items:
-                    fn(*items[q - off])
+            if item(q, NORM):
+                inverse_root(*item(q, NORM))
+            if item(q, COMBINE):
+                combine(*item(q, COMBINE))
+            if item(q, SQUARES):
+                squares(*item(q, SQUARES))
+            if needs_cover(q):
+                if q - 2 < n_steps:
+                    empty_sums(*rounds[(q - 2) // G], (q - 2) % G // 2, True)
+                if item(q, GROUP):
+                    group(*item(q, GROUP), True)
 
-            def resid_back(i, w):
-                if w == 2 and i < N_MM:
-                    stage_back_residual(i)
+            if 1 <= q <= n_steps:
+                add_layers(*rounds[(q - 1) // G], (q - 1) % G, 0)
+            if 2 * q in mix_at:
+                mix_sets(*mix_at[2 * q])
+            if 1 <= q <= n_steps:
+                add_layers(*rounds[(q - 1) // G], (q - 1) % G, 1)
+            if q < n_steps:
+                n_vec = VEC_LAYERS_FIRST if q == 0 else VEC_LAYERS_WEIGHTS if q < piece_step[-1] else VEC_LAYERS
+                products(*rounds[q // G], q % G, n_vec)
 
-            def resid_last(i, w):
-                if w == 2 and TL and i == last:
-                    stage_back_residual(i)
-                    stage_residual(i)
-
-            def resid(i, w):
-                if w == 2 and not (TL and i == last):
-                    stage_residual(i)
-
-            def stages():
-                at("rstd", stage_rstd)
-                at("mix", stage_mix)
-                at("norm", stage_norm)
-                at("group", stage_group)
-                at("quant", stage_quantize)
-                at("turn", stage_turn)
-                at("back", stage_back)
-                at("rback", resid_back)
-                at("resid", resid)
-                at("proj", stage_project)
-                at("rlast", resid_last)
-                at("sq", stage_squares)
-                at("rstd2", stage_rstd)
-
-            phase = "A"
-            for c in range(2):
-                if 1 <= q <= n_mix:
-                    pr, pg = divmod(q - 1, 4)
-                    add_layers(*rounds[pr], pg, c)
-                if c == 0:
-                    for n in parts.get(2 * q, []):
-                        mix_part(n)
-            stages()
-            if q == 6:
-                nc.vector.tensor_scalar(out=neg_scale[:], in0=scale_sb[:].rearrange("p h j -> p (h j)"), scalar1=-1.0,
-                                        scalar2=None, op0=ALU.mult)
-            if q < n_mix:
-                products(*rounds[r], g, VH if q < 1 else VT if q >= 60 else VA if q < 13 else VB if q < 23 else VC if q < PE else VD, q)
-            phase = "B"
-            for ch in range(8 * N_MM):
-                if last_q[ch] == q - 1:
-                    empty_chunk(ch // 8, ch % 8)
-            stages()
+            for ch in chunk_last:
+                if chunk_last[ch] == q - 1:
+                    empty_chunk(*ch)
+            if last_way(q, PROJECT) is not None:
+                add_residual(last_way(q, PROJECT))
+            if item(q, GROUP) and not needs_cover(q):
+                group(*item(q, GROUP), False)
             if q - 1 in depth:
                 depth_copy(depth[q - 1])
             if q - 3 in depth:
                 depth_bias(depth[q - 3])
-            if 2 <= q <= n_mix and q % 2 == 0:
-                pr, pg = divmod(q - 1, 4)
-                empty_sums(*rounds[pr], pg // 2)
-            phase = "C"
-            for n in parts.get(2 * q + 1, []):
-                mix_part(n)
-            stages()
+            if 2 <= q <= n_steps and q % 2 == 0 and not needs_cover(q + 1):
+                empty_sums(*rounds[(q - 1) // G], (q - 1) % G // 2, False)
+
+            if 2 * q + 1 in mix_at:
+                mix_sets(*mix_at[2 * q + 1])
+            if item(q, TURN):
+                turn(*item(q, TURN))
+            if item(q, 0):
+                turn_back(*item(q, 0))
+            if item(q, PROJECT):
+                project(*item(q, PROJECT))
+            if last_way(q, GROUP) is not None and last_way(q, GROUP) < N_MM:
+                turn_back(last_way(q, GROUP), RESID)
             if q in depth:
                 depth_turn(depth[q])
             if q - 2 in depth:
                 depth_matmul(depth[q - 2])
-            phase = "D"
-            stages()
-            if q < 60 and not (TL and el == last):
-                cum = lambda t: 32 * (CE * ((t + 1) // 2) + (6 - CE) * (t // 2)) // 36
-                for s in range(cum(tq), cum(tq + 1)):
-                    chain(el, s // G, s % G)
-            phase = "E"
-            stages()
-            if 2 <= q <= 13:
-                s = q - 2
-                quantize_weight(s // 4, s % 4 // 2, s % 2)
-            if 1 + HD <= q <= 12:
-                s = q - 1
-                interleave_weight(s // 4, s % 4 // 2, s % 2)
-            if 8 <= q <= 11:
-                widen_wv((q - 8) // 2, q % 2)
-            for ch in range(8 * N_MM):
-                if first_q[ch] - WD == q:
-                    widen_chunk(ch // 8, ch % 8)
-                if ch % 2 == 0 and first_q[ch] - BD == q:
-                    build_diag(ch // 8, ch % 8 // 2)
+
+            if q < n_steps:
+                i, w = rounds[q // G]
+                nth = G * w + q % G
+                for s in range(L * G * nth // 12, L * G * (nth + 1) // 12):
+                    chain(i, s // G, s % G)
+            if item(q, NORM):
+                norm(*item(q, NORM))
+            if item(q, GROUP):
+                quantize(*item(q, GROUP))
+            if q - 1 in piece_step:
+                quantize_weight(*pieces[piece_step.index(q - 1)])
+            if q in piece_step:
+                interleave_weight(*pieces[piece_step.index(q)])
+            if q + 1 in piece_step[10:]:
+                widen_wv(*pieces[piece_step.index(q + 1)][1:])
+            for ch in chunk_first:
+                if chunk_first[ch] - WIDEN_LEAD == q:
+                    widen_chunk(*ch)
+                    if ch[1] % 2 == 0:
+                        build_diag(ch[0], ch[1] // 2)

@@ -28,7 +28,7 @@ TOK = P // L
 SETS = P // TOK
 RESID = W - 1
 
-VEC_LAYERS_FIRST, VEC_LAYERS_WEIGHTS, VEC_LAYERS = 5, 1, 2
+VEC_LAYERS_FIRST, VEC_LAYERS_WEIGHTS, VEC_LAYERS = 5, 2, 3
 WEIGHT_STEPS = 18
 MM_STEPS = (10, 18, 34, 50)
 

from contextlib import ExitStack

import concourse.mybir as mybir
from concourse.masks import make_identity

L, T, D = 8, 1024, 1024
G, W = 4, 4
C = D // G
M = W * L * G
EPS = 1e-6
FLOPS = 2 * T * D * (3 * D + M) + 2 * W * L * T * D

F32 = mybir.dt.float32
BF16 = mybir.dt.bfloat16
U32 = mybir.dt.uint32
U8 = mybir.dt.uint8
FP8 = mybir.dt.float8_e4m3fn
FP8X4 = mybir.dt.float8_e4m3fn_x4
ALU = mybir.AluOpType
ACT = mybir.ActivationFunctionType
AX = mybir.AxisListType

P = 128
HALF = 512
CHUNKS = D // P
N_MM, N_PR = 3, 5
TOK = P // L
SETS = P // TOK
RESID = W - 1

VEC_LAYERS_FIRST, VEC_LAYERS_WEIGHTS, VEC_LAYERS = 5, 2, 3
WEIGHT_STEPS = 18
MM_STEPS = (10, 18, 34, 50)

SQUARES, NORM, TURN, GROUP, PROJECT, COMBINE = 1, 2, 3, 4, 5, 6
ROUND_TO_ITEM = 5
LAST_STATE_LEAD, STATES_LEAD, DEPTH_LEAD, DEPTH_LEAD_MM = 8, 6, 5, 9
WEIGHT_LEAD, BYTES_LEAD, SETS_LEAD, WIDEN_LEAD = 2, 4, 4, 2


def tile_muddmultiwaydensegate_kernel(tc, past, wa, bb, gz, wq, wk, wv_bytes, wv_scale, out):
    nc = tc.nc
    xs = past.rearrange("l b s d -> l (b s) d")
    rows = out.rearrange("b s d -> (b s) d")

    with ExitStack() as ctx:
        keep = ctx.enter_context(tc.tile_pool(name="keep", bufs=1))
        work = ctx.enter_context(tc.tile_pool(name="work", bufs=2))
        psum = ctx.enter_context(tc.psum_pool(name="psum", bufs=8))
        ctx.enter_context(tc.manual_schedule())

        def bank(shape, dtype=F32):
            return psum.tile(shape, dtype, name="bank")

        def copy_out(on_vector, dst, src):
            if on_vector:
                nc.vector.tensor_copy(out=dst, in_=src)
            else:
                nc.scalar.copy(out=dst, in_=src)

        def half(c):
            return slice(c * HALF, (c + 1) * HALF)

        states, depth_part, dw = {}, {}, {}
        w_raw, wv_raw, w_grouped, w_mx = {}, {}, {}, {}
        coef, diag, set_raw, set_wide, mm_bank, zt_mm = {}, {}, {}, {}, {}, {}
        prods, sum_bank, zt_pr, chain_acc = {}, {}, {}, {}
        z_bank, sq_sum, rstd, n_words, nt_bank, n_grouped, n_mx, proj_bank, term = {}, {}, {}, {}, {}, {}, {}, {}, {}

        def load_state(i, l):
            x = work.tile([P, D], BF16, name="state", bufs=2 * L + 2)
            nc.sync.dma_start(out=x[:], in_=xs[l, i * P:(i + 1) * P, :])
            states[i, l] = x

        def load_weight(w, h, c):
            raw = work.tile([P, 4, HALF], BF16, name="raw", bufs=4)
            nc.sync.dma_start(out=raw[:], in_=(wq, wk)[w][half(h), half(c)].rearrange("(p j) n -> p j n", j=4))
            w_raw[w, h, c] = raw

        def load_wv(h):
            codes_in = work.tile([P, 4 * D], U8, name="wv_in")
            nc.sync.dma_start(out=codes_in[:], in_=wv_bytes[half(h), :].rearrange("(p j) n -> p (j n)", j=4))
            wv_raw[h] = codes_in

        def load_sets(i, g):
            raw = work.tile([P, SETS, C], BF16, name="raw", bufs=4)
            for u in range(SETS):
                tokens = slice(i * P + u * TOK, i * P + (u + 1) * TOK)
                nc.sync.dma_start(out=raw[:, u, :], in_=xs[:, tokens, g * C:(g + 1) * C].rearrange("l t d -> t l d"))
            set_raw[i, g] = raw

        def widen_wv(h, c):
            planes = work.tile([P, 4, HALF], BF16, name="stage", align_bytes=64, bufs=4)
            for j in range(4):
                col = j * D + c * HALF
                nc.scalar.activation(out=planes[:, j, :], in_=wv_raw[h][:, col:col + HALF].bitcast(FP8),
                                     func=ACT.Copy, scale=neg_scale[:, 4 * h + j:4 * h + j + 1])
            w_raw[2, h, c] = planes

        def interleave_weight(w, h, c):
            grouped = work.tile([P, HALF, 4], BF16, name="stage", align_bytes=64, bufs=4)
            nc.vector.tensor_copy(out=grouped[:].rearrange("p (n i) j -> p n j i", i=4),
                                  in_=w_raw[w, h, c][:].rearrange("p j (n i) -> p n j i", i=4))
            w_grouped[w, h, c] = grouped

        def quantize_weight(w, h, c):
            codes = keep.tile([P, HALF], U32, name="w_codes_%d%d%d" % (w, h, c), align_bytes=64)
            scales = keep.tile([P, HALF], U8, name="w_scales_%d%d%d" % (w, h, c), align_bytes=64)
            nc.vector.quantize_mx(out=codes[:].bitcast(FP8X4), scales=scales[:],
                                  in_=w_grouped[w, h, c][:].rearrange("p n j -> p (n j)"))
            w_mx[w, h, c] = (codes, scales)

        def depth_turn(i):
            ps = bank([P, CHUNKS, P], BF16)
            for j in range(CHUNKS):
                nc.tensor.transpose(ps[:, j, :], states[i, L - 1][:, j * P:(j + 1) * P], ident_bf[:])
            depth_part[i] = ps

        def depth_copy(i):
            last_t = work.tile([P, CHUNKS, P], BF16, name="last_t", bufs=1)
            nc.scalar.copy(out=last_t[:], in_=depth_part[i][:])
            depth_part[i] = last_t

        def depth_matmul(i):
            ps = bank([P, M])
            for j in range(CHUNKS):
                nc.tensor.matmul(ps[:], lhsT=depth_part[i][:, j, :], rhs=wa_sb[:, j, :],
                                 start=(j == 0), stop=(j == CHUNKS - 1))
            depth_part[i] = ps

        def depth_bias(i):
            d = work.tile([P, M], F32, name="dw", bufs=3)
            if i >= N_MM:
                nc.vector.tensor_tensor(out=d[:], in0=depth_part[i][:], in1=bias[:], op=ALU.add)
            else:
                nc.vector.tensor_tensor(out=d[:].rearrange("p (s w) -> p s w", w=W),
                                        in0=depth_part[i][:].rearrange("p (w s) -> p s w", w=W),
                                        in1=bias[:].rearrange("p (w s) -> p s w", w=W), op=ALU.add)
            dw[i] = d

        def parking(i):
            return rows[i * P:i * P + P * M // D, :].rearrange("a (b m) -> (a b) m", m=M)

        def park_weights(i):
            nc.sync.dma_start(out=parking(i), in_=dw[i][:])

        def fetch_weights(i):
            cf = work.tile([P, SETS, G * W], F32, name="coef")
            nc.sync.dma_start(out=cf[:], in_=parking(i).rearrange("(u t) (l x) -> (t l) u x", t=TOK, l=L))
            coef[i] = cf

        def build_diag(i, g):
            shape = [P, SETS, TOK, W]
            dg = work.tile(shape, F32, name="diag")
            nc.vector.tensor_tensor(out=dg[:], in0=coef[i][:, :, g * W:(g + 1) * W].unsqueeze(2).to_broadcast(shape),
                                    in1=own_token[:].unsqueeze(1).unsqueeze(3).to_broadcast(shape), op=ALU.mult)
            diag[i, g] = dg

        def widen_chunk(i, j):
            wide = work.tile([P, SETS, P], F32, name="stage", align_bytes=64, bufs=4)
            col = (j % 2) * P
            nc.vector.tensor_copy(out=wide[:], in_=set_raw[i, j // 2][:, :, col:col + P])
            set_wide[i, j] = wide

        def mix_sets(i, j, part):
            if part == 0:
                mm_bank[i, j] = bank([P, SETS, TOK * W])
                if j == 0:
                    zt_mm[i] = work.tile([P, W, CHUNKS, P], F32, name="zt_mm")
            for u in range(part * SETS // 2, (part + 1) * SETS // 2):
                nc.tensor.matmul(mm_bank[i, j][:, u, :], lhsT=set_wide[i, j][:, u, :],
                                 rhs=diag[i, j // 2][:, u, :, :].rearrange("p t w -> p (t w)"), start=True, stop=True)

        def empty_chunk(i, j):
            nc.scalar.copy(out=zt_mm[i][:, :, j, :], in_=mm_bank[i, j][:].rearrange("p u (t w) -> p w (u t)", w=W))

        def products(i, w, g, n_vec):
            for l in range(L):
                pr = work.tile([P, C], F32, name="prod", bufs=20)
                col = (w * L + l) * G + g
                src = states[i, l][:, g * C:(g + 1) * C]
                if l < n_vec:
                    nc.vector.tensor_scalar(out=pr[:], in0=src, scalar1=dw[i][:, col:col + 1], scalar2=None, op0=ALU.mult)
                else:
                    nc.scalar.activation(out=pr[:], in_=src, func=ACT.Copy, scale=dw[i][:, col:col + 1])
                prods[i, w, g, l] = pr

        def add_layers(i, w, g, c):
            if g % 2 == 0 and c == 0:
                sum_bank[i, w, g // 2] = bank([P, 4, P])
            for l in range(L):
                nc.tensor.matmul(sum_bank[i, w, g // 2][:, 2 * (g % 2) + c, :], lhsT=prods[i, w, g, l][:, c * P:(c + 1) * P],
                                 rhs=ident[:], is_transpose=True, start=(l == 0), stop=(l == L - 1))

        def empty_sums(i, w, h, on_vector):
            zt = work.tile([P, 4, P], F32, name="zt_pr", bufs=3)
            copy_out(on_vector, zt[:], sum_bank[i, w, h][:])
            zt_pr[i, w, h] = zt

        def chain(i, l, g):
            if l == 0 and g == 0:
                chain_acc[i] = work.tile([P, D], F32, name="chain_acc")
            col = (RESID * L + l) * G + g
            cols = slice(g * C, (g + 1) * C)
            if l == 0:
                nc.vector.tensor_scalar(out=chain_acc[i][:, cols], in0=states[i, l][:, cols],
                                        scalar1=dw[i][:, col:col + 1], scalar2=None, op0=ALU.mult)
            else:
                nc.vector.scalar_tensor_tensor(out=chain_acc[i][:, cols], in0=states[i, l][:, cols],
                                               scalar=dw[i][:, col:col + 1], in1=chain_acc[i][:, cols],
                                               op0=ALU.mult, op1=ALU.add)

        def turn_back(i, w):
            for h in range(2):
                ps = bank([P, 4, P])
                for c in range(4):
                    src = zt_mm[i][:, w, 4 * h + c, :] if i < N_MM else zt_pr[i, w, h][:, c, :]
                    nc.tensor.transpose(ps[:, c, :], src, ident[:])
                z_bank[i, w, h] = ps[:].rearrange("t c k -> t (c k)")

        def squares(i, w):
            ss = work.tile([P, 2], F32, name="sq_sum", bufs=3)
            for h in range(2):
                sq = work.tile([P, HALF], BF16, name="sq")
                nc.scalar.activation(out=sq[:], in_=z_bank[i, w, h], func=ACT.Square, scale=D ** -0.5,
                                     accum_out=ss[:, h:h + 1])
            sq_sum[i, w] = ss

        def inverse_root(i, w):
            ms = work.tile([P, 1], F32, name="ms", bufs=3)
            nc.vector.tensor_scalar(out=ms[:], in0=sq_sum[i, w][:, 0:1], scalar1=sq_sum[i, w][:, 1:2], scalar2=EPS,
                                    op0=ALU.add, op1=ALU.add)
            r = work.tile([P, 1], F32, name="rstd", bufs=3)
            nc.gpsimd.tensor_tensor(out=r[:], in0=ms[:], in1=minus_half[:], op=ALU.pow)
            rstd[i, w] = r

        def norm(i, w):
            n = work.tile([P, 2, 2, P, 2], BF16, name="n_words")
            for h in range(2):
                for u in range(2):
                    nc.vector.scalar_tensor_tensor(
                        out=n[:, h, u, :, :],
                        in0=z_bank[i, w, h].rearrange("t (p u e) -> t u p e", u=2, e=2)[:, u, :, :],
                        scalar=rstd[i, w][:],
                        in1=gain[w][:, half(h)].rearrange("t (p u e) -> t u p e", u=2, e=2)[:, u, :, :],
                        op0=ALU.mult, op1=ALU.mult)
            n_words[i, w] = n

        def turn(i, w):
            words = n_words[i, w][:].rearrange("t h u p e -> t (h u p e)").bitcast(F32)
            ps = bank([P, 2, 2, P])
            for h in range(2):
                for u in range(2):
                    s = 2 * h + u
                    nc.tensor.transpose(ps[:, h, u, :], words[:, s * P:(s + 1) * P], ident[:])
            nt_bank[i, w] = ps

        def group(i, w, on_vector):
            grouped = work.tile([P, D], BF16, name="n_grouped", align_bytes=64)
            copy_out(on_vector, grouped[:].bitcast(F32).rearrange("p (h t u) -> p h t u", h=2, u=2),
                     nt_bank[i, w][:].rearrange("p h u t -> p h t u"))
            n_grouped[i, w] = grouped

        def quantize(i, w):
            codes = work.tile([P, 2 * P], U32, name="n_codes", align_bytes=64)
            scales = work.tile([P, 2 * P], U8, name="n_scales", align_bytes=64)
            nc.vector.quantize_mx(out=codes[:].bitcast(FP8X4), scales=scales[:], in_=n_grouped[i, w][:])
            n_mx[i, w] = (codes, scales)

        def project(i, w):
            codes, scales = n_mx[i, w]
            for c in range(2):
                ps = bank([P, HALF])
                for h in range(2):
                    nc.tensor.matmul_mx(out=ps[:], lhsT=codes[:, h * P:(h + 1) * P].bitcast(FP8X4),
                                        lhsT_scale=scales[:, h * P:(h + 1) * P],
                                        rhs=w_mx[w, h, c][0][:].bitcast(FP8X4), rhs_scale=w_mx[w, h, c][1][:],
                                        start=(h == 0), stop=(h == 1))
                proj_bank[i, w, c] = ps

        def combine(i, w):
            res = work.tile([P, D], F32, name=("gate", "key_term", "result")[w])
            term[i, w] = res
            for c in range(2):
                ps = proj_bank[i, w, c][:]
                if w == 0:
                    nc.scalar.activation(out=res[:, half(c)], in_=ps, func=ACT.Sigmoid)
                elif w == 1:
                    nc.vector.tensor_tensor(out=res[:, half(c)], in0=ps, in1=term[i, 0][:, half(c)], op=ALU.mult)
                else:
                    nc.vector.scalar_tensor_tensor(out=res[:, half(c)], in0=term[i, 0][:, half(c)], scalar=1.0, in1=ps,
                                                   op0=ALU.subtract, op1=ALU.mult)
            if w == 2:
                for c in range(2):
                    nc.vector.tensor_tensor(out=res[:, half(c)], in0=res[:, half(c)], in1=term[i, 1][:, half(c)], op=ALU.add)

        def add_residual(i):
            for c in range(2):
                z3 = z_bank[i, RESID, c] if i < N_MM else chain_acc[i][:, half(c)]
                nc.vector.tensor_tensor(out=term[i, 1][:, half(c)], in0=z3, in1=term[i, 1][:, half(c)], op=ALU.add)

        def store(i):
            for c in range(2):
                nc.sync.dma_start(out=rows[i * P:(i + 1) * P, half(c)], in_=term[i, 2][:, half(c)])

        first, second = N_MM, N_MM + 1
        rounds = [(i, w) for i in range(N_MM, N_MM + N_PR) for w in range(3)]
        rounds.remove((second, 0))
        rounds.insert(1, (second, 0))
        n_steps = G * len(rounds)
        tile_step = {i: G * rounds.index((i, 0)) for i in range(N_MM, N_MM + N_PR)}
        pieces = [(w, h, c) for w in range(3) for h in range(2) for c in range(2)]
        pieces = pieces[8:10] + pieces[:8] + pieces[10:]
        piece_step = [s * WEIGHT_STEPS // len(pieces) for s in range(len(pieces))]
        mix_at, chunk_first, chunk_last = {}, {}, {}
        for i in range(N_MM):
            for n in range(2 * CHUNKS):
                place = 2 * MM_STEPS[i] + n * (MM_STEPS[i + 1] - MM_STEPS[i]) // CHUNKS
                mix_at[place] = (i, n // 2, n % 2)
                chunk_first.setdefault((i, n // 2), place // 2)
                chunk_last[i, n // 2] = place // 2
        items = {G * r + ROUND_TO_ITEM: rounds[r] for r in range(len(rounds))}
        for i in range(N_MM):
            for w in range(3):
                items[MM_STEPS[i + 1] + 1 + G * w] = (i, w)
        depth = {max(tile_step[i] - DEPTH_LEAD, 0): i for i in range(second, N_MM + N_PR)}
        for i in range(N_MM):
            depth[max(MM_STEPS[i] - DEPTH_LEAD_MM, 2)] = i

        def item(q, stage):
            return items.get(q - stage)

        def last_way(q, stage):
            it = item(q, stage)
            return it[0] if it is not None and it[1] == 2 else None

        def needs_cover(q):
            combining = item(q, COMBINE)
            return item(q, NORM) is not None and (combining is None or combining[1] == 0)

        load_state(first, L - 1)
        wa_sb = keep.tile([P, CHUNKS, M], BF16, name="wa_sb")
        nc.sync.dma_start(out=wa_sb[:], in_=wa.rearrange("(j p) m -> p j m", p=P))
        bias = keep.tile([P, M], BF16, name="bias")
        nc.sync.dma_start(out=bias[:], in_=bb.partition_broadcast(P))
        scale_sb = keep.tile([P, 2, 4], F32, name="scale_sb")
        nc.sync.dma_start(out=scale_sb[:], in_=wv_scale.rearrange("(h p j) o -> p h (j o)", h=2, j=4))
        load_wv(0)
        load_state(second, L - 1)
        for l in range(L - 1):
            load_state(first, l)
        load_weight(*pieces[2])
        load_state(0, L - 1)
        load_weight(*pieces[3])
        gain = []
        for w in range(3):
            gain_w = keep.tile([P, D], BF16, name="gain_%d" % w)
            nc.sync.dma_start(out=gain_w[:], in_=gz[w, :].partition_broadcast(P))
            gain.append(gain_w)

        ident = keep.tile([P, P], F32, name="ident")
        make_identity(nc, ident[:])
        ident_bf = keep.tile([P, P], BF16, name="ident_bf")
        nc.vector.tensor_copy(out=ident_bf[:], in_=ident[:])
        own_token = keep.tile([P, TOK], F32, name="own_token")
        nc.vector.tensor_reduce(out=own_token[:], in_=ident[:].rearrange("p (t l) -> p t l", l=L), axis=AX.X, op=ALU.add)
        minus_half = keep.tile([P, 1], F32, name="minus_half")
        nc.gpsimd.memset(minus_half[:], -0.5)
        neg_scale = keep.tile([P, 8], F32, name="neg_scale")
        nc.vector.tensor_scalar(out=neg_scale[:], in0=scale_sb[:].rearrange("p h j -> p (h j)"), scalar1=-1.0,
                                scalar2=None, op0=ALU.mult)
        depth_turn(first)
        depth_copy(first)
        depth_matmul(first)
        widen_wv(0, 0)
        widen_wv(0, 1)
        depth_bias(first)

        for q in range(max(items) + COMBINE + 2):
            if depth.get(q - 4, N_MM) < N_MM:
                park_weights(depth[q - 4])
            if depth.get(q - 5, N_MM) < N_MM:
                fetch_weights(depth[q - 5])
            if last_way(q - 1, COMBINE) is not None:
                store(last_way(q - 1, COMBINE))
            for i in range(second, N_MM + N_PR):
                if q == tile_step[i] - LAST_STATE_LEAD:
                    load_state(i, L - 1)
                if q == max(tile_step[i] - STATES_LEAD, 0):
                    for l in range(L - 1):
                        load_state(i, l)
            for s in range(4, 10):
                if q == piece_step[s] - WEIGHT_LEAD:
                    load_weight(*pieces[s])
            if q == piece_step[10] - BYTES_LEAD:
                load_wv(1)
            if 0 < depth.get(q + 2, 0) < N_MM:
                load_state(depth[q + 2], L - 1)
            for i in range(N_MM):
                for g in range(G):
                    if q == chunk_first[i, 2 * g] - SETS_LEAD:
                        load_sets(i, g)

            if item(q, NORM):
                inverse_root(*item(q, NORM))
            if item(q, COMBINE):
                combine(*item(q, COMBINE))
            if item(q, SQUARES):
                squares(*item(q, SQUARES))
            if needs_cover(q):
                if q - 2 < n_steps:
                    empty_sums(*rounds[(q - 2) // G], (q - 2) % G // 2, True)
                if item(q, GROUP):
                    group(*item(q, GROUP), True)

            if 1 <= q <= n_steps:
                add_layers(*rounds[(q - 1) // G], (q - 1) % G, 0)
            if 2 * q in mix_at:
                mix_sets(*mix_at[2 * q])
            if 1 <= q <= n_steps:
                add_layers(*rounds[(q - 1) // G], (q - 1) % G, 1)
            if q < n_steps:
                n_vec = VEC_LAYERS_FIRST if q == 0 else VEC_LAYERS_WEIGHTS if q < piece_step[-1] else VEC_LAYERS
                products(*rounds[q // G], q % G, n_vec)

            for ch in chunk_last:
                if chunk_last[ch] == q - 1:
                    empty_chunk(*ch)
            if last_way(q, PROJECT) is not None:
                add_residual(last_way(q, PROJECT))
            if item(q, GROUP) and not needs_cover(q):
                group(*item(q, GROUP), False)
            if q - 1 in depth:
                depth_copy(depth[q - 1])
            if q - 3 in depth:
                depth_bias(depth[q - 3])
            if 2 <= q <= n_steps and q % 2 == 0 and not needs_cover(q + 1):
                empty_sums(*rounds[(q - 1) // G], (q - 1) % G // 2, False)

            if 2 * q + 1 in mix_at:
                mix_sets(*mix_at[2 * q + 1])
            if item(q, TURN):
                turn(*item(q, TURN))
            if item(q, 0):
                turn_back(*item(q, 0))
            if item(q, PROJECT):
                project(*item(q, PROJECT))
            if last_way(q, GROUP) is not None and last_way(q, GROUP) < N_MM:
                turn_back(last_way(q, GROUP), RESID)
            if q in depth:
                depth_turn(depth[q])
            if q - 2 in depth:
                depth_matmul(depth[q - 2])

            if q < n_steps:
                i, w = rounds[q // G]
                nth = G * w + q % G
                for s in range(L * G * nth // 12, L * G * (nth + 1) // 12):
                    chain(i, s // G, s % G)
            if item(q, NORM):
                norm(*item(q, NORM))
            if item(q, GROUP):
                quantize(*item(q, GROUP))
            if q - 1 in piece_step:
                quantize_weight(*pieces[piece_step.index(q - 1)])
            if q in piece_step:
                interleave_weight(*pieces[piece_step.index(q)])
            if q + 1 in piece_step[10:]:
                widen_wv(*pieces[piece_step.index(q + 1)][1:])
            for ch in chunk_first:
                if chunk_first[ch] - WIDEN_LEAD == q:
                    widen_chunk(*ch)
                    if ch[1] % 2 == 0:
                        build_diag(ch[0], ch[1] // 2)
